import numpy as np
import ml_dtypes


def mxq(x, axis, fmt="e4m3"):
    dtype, down = {"e4m3": (ml_dtypes.float8_e4m3fn, 7), "e5m2": (ml_dtypes.float8_e5m2, 14)}[fmt]
    v = np.moveaxis(np.asarray(x, np.float32).astype(ml_dtypes.bfloat16).astype(np.float64), axis, -1)
    blocks = v.reshape(v.shape[:-1] + (-1, 32))
    amax = np.abs(blocks).max(-1, keepdims=True)
    byte = np.maximum(np.where(amax > 0, np.frexp(amax)[1] - 1 + 127, 0) - down, 1)
    scale = np.exp2(byte - 127.0)
    codes = (blocks / scale).astype(np.float32).astype(dtype).astype(np.float64)
    return np.moveaxis((codes * scale).reshape(v.shape), -1, axis)


WIDE = False


def mx_kscale(k):
    if not WIDE:
        return np.ones(k)
    levels = np.array([10, -10, 5, -5, 0])
    if k % 512:
        return np.exp2(np.random.permutation(np.resize(levels, k // 32))).repeat(32)
    a = np.empty((k // 512, 16))
    for p in range(k // 512):
        a[p, :8] = np.random.permutation(np.resize(levels, 8))
        for g in range(8):
            far = levels[np.abs(levels - a[p, g]) >= 10]
            a[p, g + 8] = far[np.random.randint(len(far))]
    return np.exp2(a.ravel()).repeat(32)


def f64(x):
    return np.asarray(x).astype(np.float64)


def striped(idx):
    return np.tile(idx.reshape(-1, 16).T, (8, 1)).astype(np.uint16)


def unstriped(offs):
    return offs[:16].T.reshape(-1).astype(np.int64)


def striped8(idx):
    return np.concatenate([x.reshape(-1, 16).T for x in idx]).astype(np.uint16)


def runs(offs, k):
    lists = np.stack([offs[16 * r : 16 * r + 16].T.reshape(-1) for r in range(8)]).astype(np.int64)
    return lists[np.arange(k) % 512 // 64]


def pack_weight(w):
    k, n = w.shape
    w = f64(np.asarray(w, np.float32).astype(ml_dtypes.bfloat16)).reshape(k // 32, 32, n)
    amax = np.abs(w).max(1)
    byte = np.clip(np.where(amax > 0, np.frexp(amax)[1] - 1 + 127 - 7, 1), 1, 254)
    scaled = (w * np.exp2(127.0 - byte)[:, None, :]).reshape(k, n).astype(np.float32)
    words = np.ascontiguousarray(scaled.reshape(k // 512, 128, 4, n).transpose(0, 1, 3, 2)).astype(ml_dtypes.float8_e4m3fn).view(np.uint8)
    return words, np.ascontiguousarray(byte.astype(np.uint8).reshape(k // 512, 16, n))


def unpack_weight(words, scales):
    g, p, n, _ = words.shape
    vals = np.ascontiguousarray(words).view(ml_dtypes.float8_e4m3fn).astype(np.float64) * np.repeat(np.exp2(scales.astype(np.float64) - 127.0), 8, axis=1)[..., None]
    return vals.transpose(0, 1, 3, 2).reshape(g * 512, n)

def planes(y):
    n, m = y.shape
    v = y.astype(np.float32).astype(ml_dtypes.bfloat16).astype(np.float64).reshape(n // 32, 32, m)
    top = np.abs(v).max(1)
    byte = np.clip(np.where(top > 0, np.frexp(top)[1] - 1 + 127 - 7, 1), 1, 254)
    codes = (v * np.exp2(127.0 - byte)[:, None, :]).reshape(n, m).astype(np.float32).astype(ml_dtypes.float8_e4m3fn).view(np.uint8)
    words = codes.reshape(n // 512, 128, 4, m).transpose(0, 1, 3, 2)
    return np.ascontiguousarray(words), np.ascontiguousarray(byte.astype(np.uint8).reshape(n // 512, 16, m))


K, T, S, N, U = 512, 2048, 512, 512, 1024


def setup_inputs():
    n = np.random.standard_normal
    s = mx_kscale(K)[:, None]
    packed_xT = pack_weight(n((K, T)) * s)
    return {
        "x_words": packed_xT[0],
        "x_scales": packed_xT[1],
        "w1": (n((K, N)) / np.sqrt(K) / s).astype(np.float32),
        "par": n((N, U)).astype(np.float32),
        "m1": n((N, U)).astype(np.float32),
        "m2": np.random.uniform(0.5, 2.0, (N, U)).astype(np.float32),
        "offs": striped(np.random.permutation(T)[:S]),
        "ent": striped8(np.stack([np.random.permutation(U)[:S] for _ in range(8)])),
    }


def reference(x_words, x_scales, w1, par, m1, m2, offs, ent):
    xq = unpack_weight(x_words, x_scales)[:, unstriped(offs)]
    y = mxq(f64(w1), 0, "e4m3").T @ xq
    a = 0.75 * (f64(m1)[np.arange(N)[:, None], runs(ent, N)]) + 0.25 * y
    b = 0.875 * (f64(m2)[np.arange(N)[:, None], runs(ent, N)]) + 0.125 * ((y) ** 2)
    o = f64(par)[np.arange(N)[:, None], runs(ent, N)] - (0.5 * (a / np.sqrt(b)))
    out = f64(par).copy()
    out[np.arange(N)[:, None], runs(ent, N)] = o
    return (out,) + planes(out)

@@ -1,0 +1,196 @@
+import math
+from contextlib import ExitStack
+
+import concourse.mybir as mybir
+
+K, T, S, N, U = 512, 2048, 512, 512, 1024
+FLOPS = 2 * K * N * S
+
+F32 = mybir.dt.float32
+BF16 = mybir.dt.bfloat16
+I32 = mybir.dt.int32
+U32 = mybir.dt.uint32
+U16 = mybir.dt.uint16
+U8 = mybir.dt.uint8
+FP8X4 = mybir.dt.float8_e4m3fn_x4
+ALU = mybir.AluOpType
+ACT = mybir.ActivationFunctionType
+
+P = 128
+PACK = 4
+W_SPLIT = 88
+CHUNK = 256
+CHUNKS = U // CHUNK
+
+
+def tile_picked_sadam_none_po_kernel(
+    tc, x_words, x_scales, w1, par, m1, m2, offs, ent, out_0, out_1, out_2
+):
+    nc = tc.nc
+    with ExitStack() as ctx:
+        keep = ctx.enter_context(tc.tile_pool(name="keep", bufs=1))
+        psum = ctx.enter_context(tc.psum_pool(name="psum", bufs=1))
+
+        offs_t = keep.tile([P, S // 16], U16, name="offs_t")
+        ent_t = keep.tile([P, S // 16], U16, name="ent_t")
+        w_raw = keep.tile([P, PACK, N], F32, name="w_raw")
+        xw = keep.tile([P, T], I32, name="xw")
+        xs_in = keep.tile([P, T // 4], I32, name="xs_in")
+        xs = keep.tile([P, T], U8, name="xs")
+        seven = keep.tile([P, 1], F32, name="seven")
+        root = keep.tile([P, 1], F32, name="root")
+        par_t = [keep.tile([P, U], F32, name="par%d" % t) for t in range(PACK)]
+        new_t = [keep.tile([P, U], F32, name="new%d" % t) for t in range(PACK)]
+        m1_t = [keep.tile([P, U], F32, name="m1_%d" % t) for t in range(PACK)]
+        m2_t = [keep.tile([P, U], F32, name="m2_%d" % t) for t in range(PACK)]
+
+        nc.vector.memset(seven[:], 7.0)
+        nc.vector.memset(xs[:].bitcast(I32), 0)
+        nc.sync.dma_start(offs_t[:], offs)
+        for q in range(4):
+            nc.sync.dma_start(
+                out=xs_in[32 * q : 32 * q + 4, :],
+                in_=x_scales[0, 4 * q : 4 * q + 4, :].bitcast(I32),
+            )
+        nc.sync.dma_start(out=w_raw[:], in_=w1.rearrange("(p j) c -> p j c", j=PACK))
+        nc.sync.dma_start(out=xw[:], in_=x_words[0].rearrange("p c r -> p (c r)").bitcast(I32))
+        nc.sync.dma_start(ent_t[:], ent)
+        par_rows = par.rearrange("(p t) u -> p t u", t=PACK)
+        m1_rows = m1.rearrange("(p t) u -> p t u", t=PACK)
+        m2_rows = m2.rearrange("(p t) u -> p t u", t=PACK)
+        out_rows = out_0.rearrange("(p t) u -> p t u", t=PACK)
+        nc.sync.dma_start(out=par_t[0][:], in_=par_rows[:, 0, :])
+        for t in range(PACK):
+            nc.sync.dma_start(out=m1_t[t][:], in_=m1_rows[:, t, :])
+            nc.sync.dma_start(out=m2_t[t][:], in_=m2_rows[:, t, :])
+            if t > 0:
+                nc.sync.dma_start(out=new_t[t - 1][:], in_=par_rows[:, t - 1, :])
+                nc.sync.dma_start(out=par_t[t][:], in_=par_rows[:, t, :])
+        nc.sync.dma_start(out=new_t[PACK - 1][:], in_=par_rows[:, PACK - 1, :])
+
+        nc.scalar.activation(root[:], seven[:], ACT.Abs_reciprocal_sqrt)
+        for q in range(4):
+            rows = slice(32 * q, 32 * q + 4)
+            nc.vector.tensor_copy(out=xs[rows, :].bitcast(I32), in_=xs_in[rows, :])
+        xq_s = keep.tile([P, S], U8, name="xq_s", align_bytes=64)
+        nc.vector.tensor_copy(xq_s[:], xs[:].indirect(offs_t[:]))
+
+        w_bf = keep.tile([P, PACK * P * PACK], BF16, name="w_bf", align_bytes=64)
+        w_dst = w_bf[:].rearrange("p (t m j) -> p m j t", t=PACK, j=PACK)
+        w_src = w_raw[:].rearrange("p j (m t) -> p m j t", t=PACK)
+        nc.vector.tensor_copy(out=w_dst[:, :W_SPLIT], in_=w_src[:, :W_SPLIT])
+        nc.scalar.copy(out=w_dst[:, W_SPLIT:], in_=w_src[:, W_SPLIT:])
+        w_c = keep.tile([P, N], U32, name="w_c", align_bytes=64)
+        w_s = keep.tile([P, N], U8, name="w_s", align_bytes=64)
+        nc.vector.quantize_mx(out=w_c[:].bitcast(FP8X4), scales=w_s[:], in_=w_bf[:])
+
+        xq_c = keep.tile([P, S], U32, name="xq_c", align_bytes=64)
+        nc.vector.tensor_copy(xq_c[:], xw[:].bitcast(U32).indirect(offs_t[:]))
+
+        ysq = []
+        ythird = []
+        for t in range(PACK):
+            acc = psum.tile([P, S], F32, name="acc%d" % t)
+            cols = slice(t * P, (t + 1) * P)
+            nc.tensor.matmul_mx(
+                out=acc[:],
+                lhsT=w_c[:, cols].bitcast(FP8X4),
+                lhsT_scale=w_s[:, cols],
+                rhs=xq_c[:].bitcast(FP8X4),
+                rhs_scale=xq_s[:],
+                start=True,
+                stop=True,
+            )
+            sq = keep.tile([P, S], F32, name="ysq%d" % t)
+            th = keep.tile([P, S], F32, name="yth%d" % t)
+            ysq.append((acc, sq))
+            ythird.append((acc, th))
+
+        def leave_bank(t):
+            acc, th = ythird[t]
+            nc.scalar.activation(th[:], acc[:], ACT.Copy, scale=0.25 / 0.75)
+            acc, sq = ysq[t]
+            nc.scalar.activation(sq[:], acc[:], ACT.Square, scale=root[:])
+
+        a_t = [keep.tile([P, S], F32, name="a%d" % t) for t in range(PACK)]
+        b_t = [keep.tile([P, S], F32, name="b%d" % t) for t in range(PACK)]
+        r_t = [keep.tile([P, S], F32, name="r%d" % t) for t in range(PACK)]
+        g_t = [keep.tile([P, S], F32, name="g%d" % t) for t in range(PACK)]
+        u_t = [keep.tile([P, S], F32, name="u%d" % t) for t in range(PACK)]
+        y_bf = [keep.tile([P, CHUNK, PACK], BF16, name="ybf%d" % c, align_bytes=64) for c in range(CHUNKS)]
+        o_c = keep.tile([P, U], U32, name="o_c", align_bytes=64)
+        o_s = keep.tile([P, U], U8, name="o_s", align_bytes=64)
+
+        def second_moment(t):
+            nc.vector.tensor_tensor(b_t[t][:], m2_t[t][:].indirect(ent_t[:]), ysq[t][1][:], ALU.add)
+            nc.scalar.activation(r_t[t][:], b_t[t][:], ACT.Abs_reciprocal_sqrt)
+
+        def first_moment(t):
+            nc.vector.tensor_tensor(a_t[t][:], m1_t[t][:].indirect(ent_t[:]), ythird[t][1][:], ALU.add)
+
+        def old_par(t):
+            nc.vector.tensor_copy(g_t[t][:], par_t[t][:].indirect(ent_t[:]))
+
+        def step(t):
+            nc.vector.scalar_tensor_tensor(
+                u_t[t][:], a_t[t][:], -0.5 * 0.75 / math.sqrt(0.875), r_t[t][:], ALU.mult, ALU.mult
+            )
+
+        def put_back(t):
+            nc.vector.tensor_tensor(new_t[t][:].indirect(ent_t[:]), g_t[t][:], u_t[t][:], ALU.add)
+            nc.scalar.dma_start(out=out_rows[:, t, :], in_=new_t[t][:])
+
+        def round_chunk(t, c, on_vector):
+            src = new_t[t][:, c * CHUNK : (c + 1) * CHUNK]
+            if on_vector:
+                nc.vector.tensor_copy(out=y_bf[c][:, :, t], in_=src)
+            elif t == PACK - 2 and c % 2 == 0:
+                nc.scalar.copy(out=y_bf[c][:, :, t : t + 2], in_=src.unsqueeze(2).to_broadcast([P, CHUNK, 2]))
+            else:
+                nc.scalar.copy(out=y_bf[c][:, :, t], in_=src)
+
+        def quantize_chunk(c):
+            cols = slice(c * CHUNK, (c + 1) * CHUNK)
+            nc.vector.quantize_mx(
+                out=o_c[:, cols].bitcast(FP8X4),
+                scales=o_s[:, cols],
+                in_=y_bf[c][:].rearrange("p c t -> p (c t)"),
+            )
+
+        last = PACK - 1
+        leave_bank(0)
+        leave_bank(1)
+        old_par(0)
+        first_moment(0)
+        second_moment(0)
+        first_moment(1)
+        step(0)
+        leave_bank(2)
+        leave_bank(3)
+        for t in range(1, PACK):
+            second_moment(t)
+            put_back(t - 1)
+            for c in range(CHUNKS):
+                round_chunk(t - 1, c, False)
+            step(t)
+            old_par(t)
+            if t < last:
+                first_moment(t + 1)
+        put_back(last)
+
+        round_chunk(last, 1, False)
+        round_chunk(last, 3, False)
+        round_chunk(last, 0, True)
+        round_chunk(last, 2, True)
+        words = out_1[0].rearrange("p c r -> p (c r)").bitcast(I32)
+        for c in range(CHUNKS):
+            quantize_chunk(c)
+            if c % 2 == 1:
+                cols = slice((c - 1) * CHUNK, (c + 1) * CHUNK)
+                nc.sync.dma_start(out=words[:, cols], in_=o_c[:, cols].bitcast(I32))
+        for q in range(4):
+            eng = nc.scalar if q % 2 == 0 else nc.sync
+            eng.dma_start(
+                out=out_2[0, 4 * q : 4 * q + 4, :].bitcast(I32),
+                in_=o_s[32 * q : 32 * q + 4, :].bitcast(I32),
+            )

@@ -1,4 +1,3 @@
-import math
 from contextlib import ExitStack
 
 import concourse.mybir as mybir
@@ -39,7 +38,7 @@ def tile_picked_sadam_none_po_kernel(
         xs = keep.tile([P, T], U8, name="xs")
         seven = keep.tile([P, 1], F32, name="seven")
         root = keep.tile([P, 1], F32, name="root")
-        par_t = [keep.tile([P, U], F32, name="par%d" % t) for t in range(PACK)]
+        par_t = [keep.tile([P, U], F32, name="par%d" % t) for t in range(PACK - 1)]
         new_t = [keep.tile([P, U], F32, name="new%d" % t) for t in range(PACK)]
         m1_t = [keep.tile([P, U], F32, name="m1_%d" % t) for t in range(PACK)]
         m2_t = [keep.tile([P, U], F32, name="m2_%d" % t) for t in range(PACK)]
@@ -59,14 +58,24 @@ def tile_picked_sadam_none_po_kernel(
         m1_rows = m1.rearrange("(p t) u -> p t u", t=PACK)
         m2_rows = m2.rearrange("(p t) u -> p t u", t=PACK)
         out_rows = out_0.rearrange("(p t) u -> p t u", t=PACK)
-        nc.sync.dma_start(out=par_t[0][:], in_=par_rows[:, 0, :])
-        for t in range(PACK):
-            nc.sync.dma_start(out=m1_t[t][:], in_=m1_rows[:, t, :])
-            nc.sync.dma_start(out=m2_t[t][:], in_=m2_rows[:, t, :])
-            if t > 0:
-                nc.sync.dma_start(out=new_t[t - 1][:], in_=par_rows[:, t - 1, :])
-                nc.sync.dma_start(out=par_t[t][:], in_=par_rows[:, t, :])
-        nc.sync.dma_start(out=new_t[PACK - 1][:], in_=par_rows[:, PACK - 1, :])
+        def load(tiles, rows, t):
+            nc.sync.dma_start(out=tiles[t][:], in_=rows[:, t, :])
+
+        load(new_t, par_rows, 3)
+        load(m1_t, m1_rows, 0)
+        load(m2_t, m2_rows, 0)
+        load(m1_t, m1_rows, 1)
+        load(m1_t, m1_rows, 2)
+        load(par_t, par_rows, 0)
+        load(m2_t, m2_rows, 1)
+        load(new_t, par_rows, 0)
+        load(par_t, par_rows, 1)
+        load(m2_t, m2_rows, 2)
+        load(new_t, par_rows, 1)
+        load(par_t, par_rows, 2)
+        load(m1_t, m1_rows, 3)
+        load(m2_t, m2_rows, 3)
+        load(new_t, par_rows, 2)
 
         nc.scalar.activation(root[:], seven[:], ACT.Abs_reciprocal_sqrt)
         for q in range(4):
@@ -123,22 +132,25 @@ def tile_picked_sadam_none_po_kernel(
 
         def second_moment(t):
             nc.vector.tensor_tensor(b_t[t][:], m2_t[t][:].indirect(ent_t[:]), ysq[t][1][:], ALU.add)
-            nc.scalar.activation(r_t[t][:], b_t[t][:], ACT.Abs_reciprocal_sqrt)
+            nc.scalar.activation(r_t[t][:], b_t[t][:], ACT.Abs_reciprocal_sqrt, scale=0.875 / (0.5 * 0.75) ** 2)
 
         def first_moment(t):
             nc.vector.tensor_tensor(a_t[t][:], m1_t[t][:].indirect(ent_t[:]), ythird[t][1][:], ALU.add)
 
-        def old_par(t):
-            nc.vector.tensor_copy(g_t[t][:], par_t[t][:].indirect(ent_t[:]))
+        last = PACK - 1
+        a_neg = keep.tile([P, S], F32, name="a_neg")
 
-        def step(t):
-            nc.vector.scalar_tensor_tensor(
-                u_t[t][:], a_t[t][:], -0.5 * 0.75 / math.sqrt(0.875), r_t[t][:], ALU.mult, ALU.mult
-            )
+        def step(t, eng, a):
+            eng.tensor_tensor(u_t[t][:], a[:], r_t[t][:], ALU.mult)
+
+        def new_par(t):
+            nc.vector.tensor_tensor(g_t[t][:], par_t[t][:].indirect(ent_t[:]), u_t[t][:], ALU.subtract)
 
         def put_back(t):
-            nc.vector.tensor_tensor(new_t[t][:].indirect(ent_t[:]), g_t[t][:], u_t[t][:], ALU.add)
+            nc.vector.tensor_copy(new_t[t][:].indirect(ent_t[:]), g_t[t][:])
             nc.scalar.dma_start(out=out_rows[:, t, :], in_=new_t[t][:])
+            for c in range(CHUNKS):
+                round_chunk(t, c, False)
 
         def round_chunk(t, c, on_vector):
             src = new_t[t][:, c * CHUNK : (c + 1) * CHUNK]
@@ -157,26 +169,32 @@ def tile_picked_sadam_none_po_kernel(
                 in_=y_bf[c][:].rearrange("p c t -> p (c t)"),
             )
 
-        last = PACK - 1
         leave_bank(0)
         leave_bank(1)
-        old_par(0)
+        nc.vector.tensor_copy(g_t[last][:], new_t[last][:].indirect(ent_t[:]))
         first_moment(0)
         second_moment(0)
         first_moment(1)
-        step(0)
+        step(0, nc.vector, a_t[0])
         leave_bank(2)
         leave_bank(3)
-        for t in range(1, PACK):
-            second_moment(t)
-            put_back(t - 1)
-            for c in range(CHUNKS):
-                round_chunk(t - 1, c, False)
-            step(t)
-            old_par(t)
-            if t < last:
-                first_moment(t + 1)
-        put_back(last)
+        first_moment(2)
+        new_par(0)
+        second_moment(1)
+        step(1, nc.gpsimd, a_t[1])
+        put_back(0)
+        new_par(1)
+        second_moment(2)
+        step(2, nc.gpsimd, a_t[2])
+        put_back(1)
+        new_par(2)
+        first_moment(3)
+        nc.scalar.activation(a_neg[:], a_t[last][:], ACT.Copy, scale=-1.0)
+        second_moment(3)
+        step(3, nc.gpsimd, a_neg)
+        put_back(2)
+        nc.vector.tensor_tensor(new_t[last][:].indirect(ent_t[:]), g_t[last][:], u_t[last][:], ALU.add)
+        nc.sync.dma_start(out=out_rows[:, last, :], in_=new_t[last][:])
 
         round_chunk(last, 1, False)
         round_chunk(last, 3, False)

@@ -47,7 +47,8 @@ def tile_picked_sadam_none_po_kernel(
         nc.vector.memset(xs[:].bitcast(I32), 0)
         nc.sync.dma_start(offs_t[:], offs)
         for q in range(4):
-            nc.sync.dma_start(
+            eng = nc.sync if q < 2 else nc.scalar
+            eng.dma_start(
                 out=xs_in[32 * q : 32 * q + 4, :],
                 in_=x_scales[0, 4 * q : 4 * q + 4, :].bitcast(I32),
             )
@@ -96,30 +97,34 @@ def tile_picked_sadam_none_po_kernel(
         xq_c = keep.tile([P, S], U32, name="xq_c", align_bytes=64)
         nc.vector.tensor_copy(xq_c[:], xw[:].bitcast(U32).indirect(offs_t[:]))
 
-        ysq = []
-        ythird = []
+        ysq = [keep.tile([P, S], F32, name="ysq%d" % t) for t in range(PACK)]
+        ythird = [keep.tile([P, S], F32, name="yth%d" % t) for t in range(PACK)]
+        banks = []
         for t in range(PACK):
-            acc = psum.tile([P, S], F32, name="acc%d" % t)
             cols = slice(t * P, (t + 1) * P)
-            nc.tensor.matmul_mx(
-                out=acc[:],
-                lhsT=w_c[:, cols].bitcast(FP8X4),
-                lhsT_scale=w_s[:, cols],
-                rhs=xq_c[:].bitcast(FP8X4),
-                rhs_scale=xq_s[:],
-                start=True,
-                stop=True,
-            )
-            sq = keep.tile([P, S], F32, name="ysq%d" % t)
-            th = keep.tile([P, S], F32, name="yth%d" % t)
-            ysq.append((acc, sq))
-            ythird.append((acc, th))
+            parts = 2 if t == 0 else 1
+            width = S // parts
+            mine = []
+            for h in range(parts):
+                acc = psum.tile([P, width], F32, name="acc%d_%d" % (t, h))
+                ents = slice(h * width, (h + 1) * width)
+                nc.tensor.matmul_mx(
+                    out=acc[:],
+                    lhsT=w_c[:, cols].bitcast(FP8X4),
+                    lhsT_scale=w_s[:, cols],
+                    rhs=xq_c[:, ents].bitcast(FP8X4),
+                    rhs_scale=xq_s[:, ents],
+                    start=True,
+                    stop=True,
+                )
+                mine.append((acc, ents))
+            banks.append(mine)
 
         def leave_bank(t):
-            acc, th = ythird[t]
-            nc.scalar.activation(th[:], acc[:], ACT.Copy, scale=0.25 / 0.75)
-            acc, sq = ysq[t]
-            nc.scalar.activation(sq[:], acc[:], ACT.Square, scale=root[:])
+            for acc, ents in banks[t]:
+                nc.scalar.activation(ythird[t][:, ents], acc[:], ACT.Copy, scale=0.25 / 0.75)
+            for acc, ents in banks[t]:
+                nc.scalar.activation(ysq[t][:, ents], acc[:], ACT.Square, scale=root[:])
 
         a_t = [keep.tile([P, S], F32, name="a%d" % t) for t in range(PACK)]
         b_t = [keep.tile([P, S], F32, name="b%d" % t) for t in range(PACK)]
@@ -131,11 +136,11 @@ def tile_picked_sadam_none_po_kernel(
         o_s = keep.tile([P, U], U8, name="o_s", align_bytes=64)
 
         def second_moment(t):
-            nc.vector.tensor_tensor(b_t[t][:], m2_t[t][:].indirect(ent_t[:]), ysq[t][1][:], ALU.add)
+            nc.vector.tensor_tensor(b_t[t][:], m2_t[t][:].indirect(ent_t[:]), ysq[t][:], ALU.add)
             nc.scalar.activation(r_t[t][:], b_t[t][:], ACT.Abs_reciprocal_sqrt, scale=0.875 / (0.5 * 0.75) ** 2)
 
         def first_moment(t):
-            nc.vector.tensor_tensor(a_t[t][:], m1_t[t][:].indirect(ent_t[:]), ythird[t][1][:], ALU.add)
+            nc.vector.tensor_tensor(a_t[t][:], m1_t[t][:].indirect(ent_t[:]), ythird[t][:], ALU.add)
 
         last = PACK - 1
         a_neg = keep.tile([P, S], F32, name="a_neg")
@@ -148,7 +153,7 @@ def tile_picked_sadam_none_po_kernel(
 
         def put_back(t):
             nc.vector.tensor_copy(new_t[t][:].indirect(ent_t[:]), g_t[t][:])
-            nc.scalar.dma_start(out=out_rows[:, t, :], in_=new_t[t][:])
+            nc.sync.dma_start(out=out_rows[:, t, :], in_=new_t[t][:])
             for c in range(CHUNKS):
                 round_chunk(t, c, False)
 
@@ -203,8 +208,8 @@ def tile_picked_sadam_none_po_kernel(
         words = out_1[0].rearrange("p c r -> p (c r)").bitcast(I32)
         for c in range(CHUNKS):
             quantize_chunk(c)
-            if c % 2 == 1:
-                cols = slice((c - 1) * CHUNK, (c + 1) * CHUNK)
+            if c > 0:
+                cols = slice((0 if c == 1 else c) * CHUNK, (c + 1) * CHUNK)
                 nc.sync.dma_start(out=words[:, cols], in_=o_c[:, cols].bitcast(I32))
         for q in range(4):
             eng = nc.scalar if q % 2 == 0 else nc.sync

@@ -17,9 +17,20 @@ ACT = mybir.ActivationFunctionType
 
 P = 128
 PACK = 4
+LAST = PACK - 1
+QUADRANTS = 4
+SCALE_ROWS = 4
+LIST_COLS = S // 16
 W_SPLIT = 88
-CHUNK = 256
-CHUNKS = U // CHUNK
+CHUNKS = (slice(0, 512), slice(512, 768), slice(768, 1024))
+
+
+def scale_partitions(q):
+    return slice(32 * q, 32 * q + SCALE_ROWS)
+
+
+def scale_rows(q):
+    return slice(SCALE_ROWS * q, SCALE_ROWS * (q + 1))
 
 
 def tile_picked_sadam_none_po_kernel(
@@ -30,15 +41,15 @@ def tile_picked_sadam_none_po_kernel(
         keep = ctx.enter_context(tc.tile_pool(name="keep", bufs=1))
         psum = ctx.enter_context(tc.psum_pool(name="psum", bufs=1))
 
-        offs_t = keep.tile([P, S // 16], U16, name="offs_t")
-        ent_t = keep.tile([P, S // 16], U16, name="ent_t")
+        offs_t = keep.tile([P, LIST_COLS], U16, name="offs_t")
+        ent_t = keep.tile([P, LIST_COLS], U16, name="ent_t")
         w_raw = keep.tile([P, PACK, N], F32, name="w_raw")
         xw = keep.tile([P, T], I32, name="xw")
         xs_in = keep.tile([P, T // 4], I32, name="xs_in")
         xs = keep.tile([P, T], U8, name="xs")
         seven = keep.tile([P, 1], F32, name="seven")
         root = keep.tile([P, 1], F32, name="root")
-        par_t = [keep.tile([P, U], F32, name="par%d" % t) for t in range(PACK - 1)]
+        par_t = [keep.tile([P, U], F32, name="par%d" % t) for t in range(LAST)]
         new_t = [keep.tile([P, U], F32, name="new%d" % t) for t in range(PACK)]
         m1_t = [keep.tile([P, U], F32, name="m1_%d" % t) for t in range(PACK)]
         m2_t = [keep.tile([P, U], F32, name="m2_%d" % t) for t in range(PACK)]
@@ -46,12 +57,9 @@ def tile_picked_sadam_none_po_kernel(
         nc.vector.memset(seven[:], 7.0)
         nc.vector.memset(xs[:].bitcast(I32), 0)
         nc.sync.dma_start(offs_t[:], offs)
-        for q in range(4):
-            eng = nc.sync if q < 2 else nc.scalar
-            eng.dma_start(
-                out=xs_in[32 * q : 32 * q + 4, :],
-                in_=x_scales[0, 4 * q : 4 * q + 4, :].bitcast(I32),
-            )
+        for q in range(QUADRANTS):
+            queue = nc.sync if q < QUADRANTS // 2 else nc.scalar
+            queue.dma_start(out=xs_in[scale_partitions(q), :], in_=x_scales[0, scale_rows(q), :].bitcast(I32))
         nc.sync.dma_start(out=w_raw[:], in_=w1.rearrange("(p j) c -> p j c", j=PACK))
         nc.sync.dma_start(out=xw[:], in_=x_words[0].rearrange("p c r -> p (c r)").bitcast(I32))
         nc.sync.dma_start(ent_t[:], ent)
@@ -59,29 +67,25 @@ def tile_picked_sadam_none_po_kernel(
         m1_rows = m1.rearrange("(p t) u -> p t u", t=PACK)
         m2_rows = m2.rearrange("(p t) u -> p t u", t=PACK)
         out_rows = out_0.rearrange("(p t) u -> p t u", t=PACK)
+
         def load(tiles, rows, t):
             nc.sync.dma_start(out=tiles[t][:], in_=rows[:, t, :])
 
-        load(new_t, par_rows, 3)
-        load(m1_t, m1_rows, 0)
+        load(new_t, par_rows, LAST)
         load(m2_t, m2_rows, 0)
-        load(m1_t, m1_rows, 1)
+        load(m1_t, m1_rows, 0)
         load(m1_t, m1_rows, 2)
-        load(par_t, par_rows, 0)
-        load(m2_t, m2_rows, 1)
-        load(new_t, par_rows, 0)
-        load(par_t, par_rows, 1)
-        load(m2_t, m2_rows, 2)
-        load(new_t, par_rows, 1)
-        load(par_t, par_rows, 2)
         load(m1_t, m1_rows, 3)
-        load(m2_t, m2_rows, 3)
-        load(new_t, par_rows, 2)
+        load(m1_t, m1_rows, 1)
+        for t in range(LAST):
+            load(par_t, par_rows, t)
+            load(m2_t, m2_rows, t + 1)
+            load(new_t, par_rows, t)
 
         nc.scalar.activation(root[:], seven[:], ACT.Abs_reciprocal_sqrt)
-        for q in range(4):
-            rows = slice(32 * q, 32 * q + 4)
-            nc.vector.tensor_copy(out=xs[rows, :].bitcast(I32), in_=xs_in[rows, :])
+
+        for q in range(QUADRANTS):
+            nc.vector.tensor_copy(out=xs[scale_partitions(q), :].bitcast(I32), in_=xs_in[scale_partitions(q), :])
         xq_s = keep.tile([P, S], U8, name="xq_s", align_bytes=64)
         nc.vector.tensor_copy(xq_s[:], xs[:].indirect(offs_t[:]))
 
@@ -97,123 +101,113 @@ def tile_picked_sadam_none_po_kernel(
         xq_c = keep.tile([P, S], U32, name="xq_c", align_bytes=64)
         nc.vector.tensor_copy(xq_c[:], xw[:].bitcast(U32).indirect(offs_t[:]))
 
-        ysq = [keep.tile([P, S], F32, name="ysq%d" % t) for t in range(PACK)]
-        ythird = [keep.tile([P, S], F32, name="yth%d" % t) for t in range(PACK)]
+        y_sq7 = [keep.tile([P, S], F32, name="ysq%d" % t) for t in range(PACK)]
+        y_3rd = [keep.tile([P, S], F32, name="yth%d" % t) for t in range(PACK)]
         banks = []
         for t in range(PACK):
-            cols = slice(t * P, (t + 1) * P)
+            features = slice(t * P, (t + 1) * P)
             parts = 2 if t == 0 else 1
             width = S // parts
-            mine = []
+            plane_banks = []
             for h in range(parts):
                 acc = psum.tile([P, width], F32, name="acc%d_%d" % (t, h))
-                ents = slice(h * width, (h + 1) * width)
+                entries = slice(h * width, (h + 1) * width)
                 nc.tensor.matmul_mx(
                     out=acc[:],
-                    lhsT=w_c[:, cols].bitcast(FP8X4),
-                    lhsT_scale=w_s[:, cols],
-                    rhs=xq_c[:, ents].bitcast(FP8X4),
-                    rhs_scale=xq_s[:, ents],
+                    lhsT=w_c[:, features].bitcast(FP8X4),
+                    lhsT_scale=w_s[:, features],
+                    rhs=xq_c[:, entries].bitcast(FP8X4),
+                    rhs_scale=xq_s[:, entries],
                     start=True,
                     stop=True,
                 )
-                mine.append((acc, ents))
-            banks.append(mine)
-
-        def leave_bank(t):
-            for acc, ents in banks[t]:
-                nc.scalar.activation(ythird[t][:, ents], acc[:], ACT.Copy, scale=0.25 / 0.75)
-            for acc, ents in banks[t]:
-                nc.scalar.activation(ysq[t][:, ents], acc[:], ACT.Square, scale=root[:])
+                plane_banks.append((acc, entries))
+            banks.append(plane_banks)
 
         a_t = [keep.tile([P, S], F32, name="a%d" % t) for t in range(PACK)]
-        b_t = [keep.tile([P, S], F32, name="b%d" % t) for t in range(PACK)]
+        b_t = [keep.tile([P, S], F32, name="b%d" % t, align_bytes=64) for t in range(PACK)]
         r_t = [keep.tile([P, S], F32, name="r%d" % t) for t in range(PACK)]
         g_t = [keep.tile([P, S], F32, name="g%d" % t) for t in range(PACK)]
         u_t = [keep.tile([P, S], F32, name="u%d" % t) for t in range(PACK)]
-        y_bf = [keep.tile([P, CHUNK, PACK], BF16, name="ybf%d" % c, align_bytes=64) for c in range(CHUNKS)]
+        y_bf = [keep.tile([P, U // 2, PACK], BF16, name="ybf0", align_bytes=64)]
         o_c = keep.tile([P, U], U32, name="o_c", align_bytes=64)
         o_s = keep.tile([P, U], U8, name="o_s", align_bytes=64)
 
-        def second_moment(t):
-            nc.vector.tensor_tensor(b_t[t][:], m2_t[t][:].indirect(ent_t[:]), ysq[t][:], ALU.add)
-            nc.scalar.activation(r_t[t][:], b_t[t][:], ACT.Abs_reciprocal_sqrt, scale=0.875 / (0.5 * 0.75) ** 2)
+        def leave_bank(t):
+            sign = -1.0 if t == LAST else 1.0
+            for acc, entries in banks[t]:
+                nc.scalar.activation(y_sq7[t][:, entries], acc[:], ACT.Square, scale=root[:])
+            for acc, entries in banks[t]:
+                nc.scalar.activation(y_3rd[t][:, entries], acc[:], ACT.Copy, scale=sign * 0.25 / 0.75)
 
         def first_moment(t):
-            nc.vector.tensor_tensor(a_t[t][:], m1_t[t][:].indirect(ent_t[:]), ythird[t][:], ALU.add)
+            nc.vector.tensor_tensor(a_t[t][:], m1_t[t][:].indirect(ent_t[:]), y_3rd[t][:], ALU.add)
 
-        last = PACK - 1
-        a_neg = keep.tile([P, S], F32, name="a_neg")
+        def second_moment(t):
+            nc.vector.tensor_tensor(b_t[t][:], m2_t[t][:].indirect(ent_t[:]), y_sq7[t][:], ALU.add)
+            nc.scalar.activation(r_t[t][:], b_t[t][:], ACT.Abs_reciprocal_sqrt, scale=0.875 / (0.5 * 0.75) ** 2)
 
-        def step(t, eng, a):
-            eng.tensor_tensor(u_t[t][:], a[:], r_t[t][:], ALU.mult)
+        def step(t, engine, moment):
+            engine.tensor_tensor(u_t[t][:], moment[:], r_t[t][:], ALU.mult)
 
         def new_par(t):
             nc.vector.tensor_tensor(g_t[t][:], par_t[t][:].indirect(ent_t[:]), u_t[t][:], ALU.subtract)
 
+        def finished(t, c):
+            return new_t[t][:, CHUNKS[c]]
+
+        def round_on_scalar(t, c):
+            if t + 1 == LAST and c == 0:
+                both = finished(t, c).unsqueeze(2).to_broadcast([P, U // 2, 2])
+                nc.scalar.copy(out=y_bf[c][:, :, t : t + 2], in_=both)
+            else:
+                nc.scalar.copy(out=y_bf[c][:, :, t], in_=finished(t, c))
+
         def put_back(t):
             nc.vector.tensor_copy(new_t[t][:].indirect(ent_t[:]), g_t[t][:])
             nc.sync.dma_start(out=out_rows[:, t, :], in_=new_t[t][:])
-            for c in range(CHUNKS):
-                round_chunk(t, c, False)
+            for c in range(len(y_bf)):
+                round_on_scalar(t, c)
 
-        def round_chunk(t, c, on_vector):
-            src = new_t[t][:, c * CHUNK : (c + 1) * CHUNK]
-            if on_vector:
-                nc.vector.tensor_copy(out=y_bf[c][:, :, t], in_=src)
-            elif t == PACK - 2 and c % 2 == 0:
-                nc.scalar.copy(out=y_bf[c][:, :, t : t + 2], in_=src.unsqueeze(2).to_broadcast([P, CHUNK, 2]))
-            else:
-                nc.scalar.copy(out=y_bf[c][:, :, t], in_=src)
+        leave_bank(0)
+        leave_bank(1)
+        nc.vector.tensor_copy(g_t[LAST][:], new_t[LAST][:].indirect(ent_t[:]))
+        second_moment(0)
+        first_moment(0)
+        step(0, nc.gpsimd, a_t[0])
+        for t in (2, 3):
+            nc.vector.tensor_copy(a_t[t][:], m1_t[t][:].indirect(ent_t[:]))
+        first_moment(1)
+        leave_bank(2)
+        leave_bank(3)
+        moments = [a_t[0], a_t[1], r_t[1], r_t[2]]
+        for t in range(LAST):
+            new_par(t)
+            second_moment(t + 1)
+            step(t + 1, nc.gpsimd, moments[t + 1])
+            if t + 2 <= LAST:
+                op = ALU.subtract if t + 2 == LAST else ALU.add
+                nc.gpsimd.tensor_tensor(moments[t + 2][:], y_3rd[t + 2][:], a_t[t + 2][:], op)
+            if t > 0:
+                y_bf.append(keep.tile([P, U // 4, PACK], BF16, name="ybf%d" % t, tag="b%d" % (t + 1), align_bytes=64))
+                for done in range(t):
+                    round_on_scalar(done, t)
+            put_back(t)
+        nc.vector.tensor_tensor(new_t[LAST][:].indirect(ent_t[:]), g_t[LAST][:], u_t[LAST][:], ALU.add)
+        nc.sync.dma_start(out=out_rows[:, LAST, :], in_=new_t[LAST][:])
 
-        def quantize_chunk(c):
-            cols = slice(c * CHUNK, (c + 1) * CHUNK)
+        for c in (1, 2):
+            round_on_scalar(LAST, c)
+        nc.vector.tensor_copy(out=y_bf[0][:, :, LAST], in_=finished(LAST, 0))
+        words = out_1[0].rearrange("p c r -> p (c r)").bitcast(I32)
+        for c in (1, 0, 2):
+            cols = CHUNKS[c]
             nc.vector.quantize_mx(
                 out=o_c[:, cols].bitcast(FP8X4),
                 scales=o_s[:, cols],
                 in_=y_bf[c][:].rearrange("p c t -> p (c t)"),
             )
-
-        leave_bank(0)
-        leave_bank(1)
-        nc.vector.tensor_copy(g_t[last][:], new_t[last][:].indirect(ent_t[:]))
-        first_moment(0)
-        second_moment(0)
-        first_moment(1)
-        step(0, nc.vector, a_t[0])
-        leave_bank(2)
-        leave_bank(3)
-        first_moment(2)
-        new_par(0)
-        second_moment(1)
-        step(1, nc.gpsimd, a_t[1])
-        put_back(0)
-        new_par(1)
-        second_moment(2)
-        step(2, nc.gpsimd, a_t[2])
-        put_back(1)
-        new_par(2)
-        first_moment(3)
-        nc.scalar.activation(a_neg[:], a_t[last][:], ACT.Copy, scale=-1.0)
-        second_moment(3)
-        step(3, nc.gpsimd, a_neg)
-        put_back(2)
-        nc.vector.tensor_tensor(new_t[last][:].indirect(ent_t[:]), g_t[last][:], u_t[last][:], ALU.add)
-        nc.sync.dma_start(out=out_rows[:, last, :], in_=new_t[last][:])
-
-        round_chunk(last, 1, False)
-        round_chunk(last, 3, False)
-        round_chunk(last, 0, True)
-        round_chunk(last, 2, True)
-        words = out_1[0].rearrange("p c r -> p (c r)").bitcast(I32)
-        for c in range(CHUNKS):
-            quantize_chunk(c)
-            if c > 0:
-                cols = slice((0 if c == 1 else c) * CHUNK, (c + 1) * CHUNK)
-                nc.sync.dma_start(out=words[:, cols], in_=o_c[:, cols].bitcast(I32))
-        for q in range(4):
-            eng = nc.scalar if q % 2 == 0 else nc.sync
-            eng.dma_start(
-                out=out_2[0, 4 * q : 4 * q + 4, :].bitcast(I32),
-                in_=o_s[32 * q : 32 * q + 4, :].bitcast(I32),
-            )
+            nc.sync.dma_start(out=words[:, cols], in_=o_c[:, cols].bitcast(I32))
+        for q in range(QUADRANTS):
+            queue = nc.scalar if q % 2 == 0 else nc.sync
+            queue.dma_start(out=out_2[0, scale_rows(q), :].bitcast(I32), in_=o_s[scale_partitions(q), :].bitcast(I32))

@@ -44,25 +44,26 @@ def tile_picked_sadam_none_po_kernel(
         offs_t = keep.tile([P, LIST_COLS], U16, name="offs_t")
         ent_t = keep.tile([P, LIST_COLS], U16, name="ent_t")
         w_raw = keep.tile([P, PACK, N], F32, name="w_raw")
-        xw = keep.tile([P, T], I32, name="xw")
-        xs_in = keep.tile([P, T // 4], I32, name="xs_in")
         xs = keep.tile([P, T], U8, name="xs")
-        seven = keep.tile([P, 1], F32, name="seven")
         root = keep.tile([P, 1], F32, name="root")
-        par_t = [keep.tile([P, U], F32, name="par%d" % t) for t in range(LAST)]
-        new_t = [keep.tile([P, U], F32, name="new%d" % t) for t in range(PACK)]
-        m1_t = [keep.tile([P, U], F32, name="m1_%d" % t) for t in range(PACK)]
-        m2_t = [keep.tile([P, U], F32, name="m2_%d" % t) for t in range(PACK)]
-
-        nc.vector.memset(seven[:], 7.0)
         nc.vector.memset(xs[:].bitcast(I32), 0)
-        nc.sync.dma_start(offs_t[:], offs)
-        for q in range(QUADRANTS):
-            queue = nc.sync if q < QUADRANTS // 2 else nc.scalar
-            queue.dma_start(out=xs_in[scale_partitions(q), :], in_=x_scales[0, scale_rows(q), :].bitcast(I32))
+        with tc.tile_pool(name="head", bufs=1) as head:
+            seven = head.tile([P, 1], F32, name="seven")
+            nc.vector.memset(seven[:], 7.0)
+            nc.scalar.activation(root[:], seven[:], ACT.Abs_reciprocal_sqrt)
+        tables = ctx.enter_context(tc.tile_pool(name="tables", bufs=1))
+        xw = tables.tile([P, T], I32, name="xw")
+        par_t = [tables.tile([P, U], F32, name="par%d" % t) for t in range(LAST)]
+        new_t = [tables.tile([P, U], F32, name="new%d" % t) for t in range(PACK)]
+        m1_t = [tables.tile([P, U], F32, name="m1_%d" % t) for t in range(PACK)]
+        m2_t = [tables.tile([P, U], F32, name="m2_%d" % t) for t in range(PACK)]
+
         nc.sync.dma_start(out=w_raw[:], in_=w1.rearrange("(p j) c -> p j c", j=PACK))
-        nc.sync.dma_start(out=xw[:], in_=x_words[0].rearrange("p c r -> p (c r)").bitcast(I32))
+        nc.sync.dma_start(offs_t[:], offs)
         nc.sync.dma_start(ent_t[:], ent)
+        for q in range(QUADRANTS):
+            nc.sync.dma_start(out=xs[scale_partitions(q), :].bitcast(I32), in_=x_scales[0, scale_rows(q), :].bitcast(I32))
+        nc.sync.dma_start(out=xw[:], in_=x_words[0].rearrange("p c r -> p (c r)").bitcast(I32))
         par_rows = par.rearrange("(p t) u -> p t u", t=PACK)
         m1_rows = m1.rearrange("(p t) u -> p t u", t=PACK)
         m2_rows = m2.rearrange("(p t) u -> p t u", t=PACK)
@@ -82,10 +83,7 @@ def tile_picked_sadam_none_po_kernel(
             load(m2_t, m2_rows, t + 1)
             load(new_t, par_rows, t)
 
-        nc.scalar.activation(root[:], seven[:], ACT.Abs_reciprocal_sqrt)
 
-        for q in range(QUADRANTS):
-            nc.vector.tensor_copy(out=xs[scale_partitions(q), :].bitcast(I32), in_=xs_in[scale_partitions(q), :])
         xq_s = keep.tile([P, S], U8, name="xq_s", align_bytes=64)
         nc.vector.tensor_copy(xq_s[:], xs[:].indirect(offs_t[:]))
 

@@ -21,7 +21,7 @@ LAST = PACK - 1
 QUADRANTS = 4
 SCALE_ROWS = 4
 LIST_COLS = S // 16
-W_SPLIT = 88
+W_SPLIT = 104
 CHUNKS = (slice(0, 512), slice(512, 768), slice(768, 1024))
 
 
@@ -97,7 +97,10 @@ def tile_picked_sadam_none_po_kernel(
         nc.vector.quantize_mx(out=w_c[:].bitcast(FP8X4), scales=w_s[:], in_=w_bf[:])
 
         xq_c = keep.tile([P, S], U32, name="xq_c", align_bytes=64)
-        nc.vector.tensor_copy(xq_c[:], xw[:].bitcast(U32).indirect(offs_t[:]))
+        for h in range(2):
+            half = slice(h * S // 2, (h + 1) * S // 2)
+            half_list = slice(h * LIST_COLS // 2, (h + 1) * LIST_COLS // 2)
+            nc.vector.tensor_copy(xq_c[:, half], xw[:].bitcast(U32).indirect(offs_t[:, half_list]))
 
         y_sq7 = [keep.tile([P, S], F32, name="ysq%d" % t) for t in range(PACK)]
         y_3rd = [keep.tile([P, S], F32, name="yth%d" % t) for t in range(PACK)]
@@ -178,14 +181,14 @@ def tile_picked_sadam_none_po_kernel(
         first_moment(1)
         leave_bank(2)
         leave_bank(3)
-        moments = [a_t[0], a_t[1], r_t[1], r_t[2]]
+        moments = [a_t[0], a_t[1], y_sq7[1], y_sq7[2]]
         for t in range(LAST):
             new_par(t)
             second_moment(t + 1)
-            step(t + 1, nc.gpsimd, moments[t + 1])
             if t + 2 <= LAST:
                 op = ALU.subtract if t + 2 == LAST else ALU.add
                 nc.gpsimd.tensor_tensor(moments[t + 2][:], y_3rd[t + 2][:], a_t[t + 2][:], op)
+            step(t + 1, nc.gpsimd, moments[t + 1])
             if t > 0:
                 y_bf.append(keep.tile([P, U // 4, PACK], BF16, name="ybf%d" % t, tag="b%d" % (t + 1), align_bytes=64))
                 for done in range(t):

@@ -21,7 +21,8 @@ LAST = PACK - 1
 QUADRANTS = 4
 SCALE_ROWS = 4
 LIST_COLS = S // 16
-W_SPLIT = 104
+TOP = 112
+W_SPLIT = (64, 88)
 CHUNKS = (slice(0, 512), slice(512, 768), slice(768, 1024))
 
 
@@ -43,27 +44,36 @@ def tile_picked_sadam_none_po_kernel(
 
         offs_t = keep.tile([P, LIST_COLS], U16, name="offs_t")
         ent_t = keep.tile([P, LIST_COLS], U16, name="ent_t")
-        w_raw = keep.tile([P, PACK, N], F32, name="w_raw")
-        xs = keep.tile([P, T], U8, name="xs")
+        xw = keep.tile([P, T], I32, name="xw")
+        w_raw = [keep.tile([P, 2, N], F32, name="w_raw%d" % h) for h in range(2)]
+        xg_s = keep.tile([P, S], U8, name="xg_s", align_bytes=64)
+        xq_s = keep.tile([P, S], U8, name="xq_s", align_bytes=64)
+        seven = keep.tile([P, 1], F32, name="seven")
         root = keep.tile([P, 1], F32, name="root")
-        nc.vector.memset(xs[:].bitcast(I32), 0)
+        w_rows = w1.rearrange("(p j) c -> p j c", j=PACK)
+
         with tc.tile_pool(name="head", bufs=1) as head:
-            seven = head.tile([P, 1], F32, name="seven")
+            xs = head.tile([P, T], U8, name="xs")
+            nc.sync.dma_start(offs_t[:], offs)
+            nc.sync.dma_start(out=xs[TOP:, :].bitcast(I32), in_=x_scales[0].bitcast(I32))
+            nc.sync.dma_start(out=xw[:], in_=x_words[0].rearrange("p c r -> p (c r)").bitcast(I32))
+            for h in range(2):
+                nc.sync.dma_start(out=w_raw[h][:], in_=w_rows[:, 2 * h : 2 * h + 2, :])
+            nc.sync.dma_start(ent_t[:], ent)
+            nc.vector.memset(xs[:TOP, :].bitcast(I32), 0)
             nc.vector.memset(seven[:], 7.0)
+            nc.vector.memset(xq_s[:].bitcast(I32), 0)
             nc.scalar.activation(root[:], seven[:], ACT.Abs_reciprocal_sqrt)
+            nc.vector.tensor_copy(xg_s[:], xs[:].indirect(offs_t[:]))
+        for q in range(QUADRANTS):
+            picked = slice(TOP + SCALE_ROWS * q, TOP + SCALE_ROWS * (q + 1))
+            nc.sync.dma_start(out=xq_s[scale_partitions(q), :].bitcast(I32), in_=xg_s[picked, :].bitcast(I32))
+
         tables = ctx.enter_context(tc.tile_pool(name="tables", bufs=1))
-        xw = tables.tile([P, T], I32, name="xw")
         par_t = [tables.tile([P, U], F32, name="par%d" % t) for t in range(LAST)]
         new_t = [tables.tile([P, U], F32, name="new%d" % t) for t in range(PACK)]
         m1_t = [tables.tile([P, U], F32, name="m1_%d" % t) for t in range(PACK)]
         m2_t = [tables.tile([P, U], F32, name="m2_%d" % t) for t in range(PACK)]
-
-        nc.sync.dma_start(out=w_raw[:], in_=w1.rearrange("(p j) c -> p j c", j=PACK))
-        nc.sync.dma_start(offs_t[:], offs)
-        nc.sync.dma_start(ent_t[:], ent)
-        for q in range(QUADRANTS):
-            nc.sync.dma_start(out=xs[scale_partitions(q), :].bitcast(I32), in_=x_scales[0, scale_rows(q), :].bitcast(I32))
-        nc.sync.dma_start(out=xw[:], in_=x_words[0].rearrange("p c r -> p (c r)").bitcast(I32))
         par_rows = par.rearrange("(p t) u -> p t u", t=PACK)
         m1_rows = m1.rearrange("(p t) u -> p t u", t=PACK)
         m2_rows = m2.rearrange("(p t) u -> p t u", t=PACK)
@@ -83,24 +93,23 @@ def tile_picked_sadam_none_po_kernel(
             load(m2_t, m2_rows, t + 1)
             load(new_t, par_rows, t)
 
-
-        xq_s = keep.tile([P, S], U8, name="xq_s", align_bytes=64)
-        nc.vector.tensor_copy(xq_s[:], xs[:].indirect(offs_t[:]))
+        xq_c = keep.tile([P, S], U32, name="xq_c", align_bytes=64)
+        nc.vector.tensor_copy(xq_c[:], xw[:].bitcast(U32).indirect(offs_t[:]))
 
         w_bf = keep.tile([P, PACK * P * PACK], BF16, name="w_bf", align_bytes=64)
         w_dst = w_bf[:].rearrange("p (t m j) -> p m j t", t=PACK, j=PACK)
-        w_src = w_raw[:].rearrange("p j (m t) -> p m j t", t=PACK)
-        nc.vector.tensor_copy(out=w_dst[:, :W_SPLIT], in_=w_src[:, :W_SPLIT])
-        nc.scalar.copy(out=w_dst[:, W_SPLIT:], in_=w_src[:, W_SPLIT:])
+        for h in range(2):
+            w_src = w_raw[h][:].rearrange("p j (m t) -> p m j t", t=PACK)
+            pair = slice(2 * h, 2 * h + 2)
+            nc.vector.tensor_copy(out=w_dst[:, : W_SPLIT[h], pair], in_=w_src[:, : W_SPLIT[h]])
+            nc.scalar.copy(out=w_dst[:, W_SPLIT[h] :, pair], in_=w_src[:, W_SPLIT[h] :])
         w_c = keep.tile([P, N], U32, name="w_c", align_bytes=64)
         w_s = keep.tile([P, N], U8, name="w_s", align_bytes=64)
-        nc.vector.quantize_mx(out=w_c[:].bitcast(FP8X4), scales=w_s[:], in_=w_bf[:])
-
-        xq_c = keep.tile([P, S], U32, name="xq_c", align_bytes=64)
         for h in range(2):
-            half = slice(h * S // 2, (h + 1) * S // 2)
-            half_list = slice(h * LIST_COLS // 2, (h + 1) * LIST_COLS // 2)
-            nc.vector.tensor_copy(xq_c[:, half], xw[:].bitcast(U32).indirect(offs_t[:, half_list]))
+            cols = slice(h * N // 2, (h + 1) * N // 2)
+            nc.vector.quantize_mx(
+                out=w_c[:, cols].bitcast(FP8X4), scales=w_s[:, cols], in_=w_bf[:, PACK * cols.start : PACK * cols.stop]
+            )
 
         y_sq7 = [keep.tile([P, S], F32, name="ysq%d" % t) for t in range(PACK)]
         y_3rd = [keep.tile([P, S], F32, name="yth%d" % t) for t in range(PACK)]

@@ -22,7 +22,7 @@ QUADRANTS = 4
 SCALE_ROWS = 4
 LIST_COLS = S // 16
 TOP = 112
-W_SPLIT = (64, 88)
+W_SPLIT = 104
 CHUNKS = (slice(0, 512), slice(512, 768), slice(768, 1024))
 
 
@@ -45,20 +45,18 @@ def tile_picked_sadam_none_po_kernel(
         offs_t = keep.tile([P, LIST_COLS], U16, name="offs_t")
         ent_t = keep.tile([P, LIST_COLS], U16, name="ent_t")
         xw = keep.tile([P, T], I32, name="xw")
-        w_raw = [keep.tile([P, 2, N], F32, name="w_raw%d" % h) for h in range(2)]
+        w_raw = keep.tile([P, PACK, N], F32, name="w_raw")
         xg_s = keep.tile([P, S], U8, name="xg_s", align_bytes=64)
         xq_s = keep.tile([P, S], U8, name="xq_s", align_bytes=64)
         seven = keep.tile([P, 1], F32, name="seven")
         root = keep.tile([P, 1], F32, name="root")
-        w_rows = w1.rearrange("(p j) c -> p j c", j=PACK)
 
         with tc.tile_pool(name="head", bufs=1) as head:
             xs = head.tile([P, T], U8, name="xs")
             nc.sync.dma_start(offs_t[:], offs)
             nc.sync.dma_start(out=xs[TOP:, :].bitcast(I32), in_=x_scales[0].bitcast(I32))
+            nc.sync.dma_start(out=w_raw[:], in_=w1.rearrange("(p j) c -> p j c", j=PACK))
             nc.sync.dma_start(out=xw[:], in_=x_words[0].rearrange("p c r -> p (c r)").bitcast(I32))
-            for h in range(2):
-                nc.sync.dma_start(out=w_raw[h][:], in_=w_rows[:, 2 * h : 2 * h + 2, :])
             nc.sync.dma_start(ent_t[:], ent)
             nc.vector.memset(xs[:TOP, :].bitcast(I32), 0)
             nc.vector.memset(seven[:], 7.0)
@@ -93,23 +91,20 @@ def tile_picked_sadam_none_po_kernel(
             load(m2_t, m2_rows, t + 1)
             load(new_t, par_rows, t)
 
-        xq_c = keep.tile([P, S], U32, name="xq_c", align_bytes=64)
-        nc.vector.tensor_copy(xq_c[:], xw[:].bitcast(U32).indirect(offs_t[:]))
-
         w_bf = keep.tile([P, PACK * P * PACK], BF16, name="w_bf", align_bytes=64)
         w_dst = w_bf[:].rearrange("p (t m j) -> p m j t", t=PACK, j=PACK)
-        for h in range(2):
-            w_src = w_raw[h][:].rearrange("p j (m t) -> p m j t", t=PACK)
-            pair = slice(2 * h, 2 * h + 2)
-            nc.vector.tensor_copy(out=w_dst[:, : W_SPLIT[h], pair], in_=w_src[:, : W_SPLIT[h]])
-            nc.scalar.copy(out=w_dst[:, W_SPLIT[h] :, pair], in_=w_src[:, W_SPLIT[h] :])
+        w_src = w_raw[:].rearrange("p j (m t) -> p m j t", t=PACK)
+        nc.vector.tensor_copy(out=w_dst[:, :W_SPLIT], in_=w_src[:, :W_SPLIT])
+        nc.scalar.copy(out=w_dst[:, W_SPLIT:], in_=w_src[:, W_SPLIT:])
         w_c = keep.tile([P, N], U32, name="w_c", align_bytes=64)
         w_s = keep.tile([P, N], U8, name="w_s", align_bytes=64)
+        nc.vector.quantize_mx(out=w_c[:].bitcast(FP8X4), scales=w_s[:], in_=w_bf[:])
+
+        xq_c = keep.tile([P, S], U32, name="xq_c", align_bytes=64)
         for h in range(2):
-            cols = slice(h * N // 2, (h + 1) * N // 2)
-            nc.vector.quantize_mx(
-                out=w_c[:, cols].bitcast(FP8X4), scales=w_s[:, cols], in_=w_bf[:, PACK * cols.start : PACK * cols.stop]
-            )
+            half = slice(h * S // 2, (h + 1) * S // 2)
+            half_list = slice(h * LIST_COLS // 2, (h + 1) * LIST_COLS // 2)
+            nc.vector.tensor_copy(xq_c[:, half], xw[:].bitcast(U32).indirect(offs_t[:, half_list]))
 
         y_sq7 = [keep.tile([P, S], F32, name="ysq%d" % t) for t in range(PACK)]
         y_3rd = [keep.tile([P, S], F32, name="yth%d" % t) for t in range(PACK)]

@@ -18,16 +18,17 @@ ACT = mybir.ActivationFunctionType
 P = 128
 PACK = 4
 LAST = PACK - 1
-QUADRANTS = 4
+QUADRANT = 32
+QUADRANTS = P // QUADRANT
 SCALE_ROWS = 4
+TOP = P - QUADRANTS * SCALE_ROWS
 LIST_COLS = S // 16
-TOP = 112
 W_SPLIT = 104
 CHUNKS = (slice(0, 512), slice(512, 768), slice(768, 1024))
 
 
 def scale_partitions(q):
-    return slice(32 * q, 32 * q + SCALE_ROWS)
+    return slice(QUADRANT * q, QUADRANT * q + SCALE_ROWS)
 
 
 def scale_rows(q):
@@ -152,8 +153,8 @@ def tile_picked_sadam_none_po_kernel(
             nc.vector.tensor_tensor(b_t[t][:], m2_t[t][:].indirect(ent_t[:]), y_sq7[t][:], ALU.add)
             nc.scalar.activation(r_t[t][:], b_t[t][:], ACT.Abs_reciprocal_sqrt, scale=0.875 / (0.5 * 0.75) ** 2)
 
-        def step(t, engine, moment):
-            engine.tensor_tensor(u_t[t][:], moment[:], r_t[t][:], ALU.mult)
+        def step(t, moment):
+            nc.gpsimd.tensor_tensor(u_t[t][:], moment[:], r_t[t][:], ALU.mult)
 
         def new_par(t):
             nc.vector.tensor_tensor(g_t[t][:], par_t[t][:].indirect(ent_t[:]), u_t[t][:], ALU.subtract)
@@ -163,8 +164,10 @@ def tile_picked_sadam_none_po_kernel(
 
         def round_on_scalar(t, c):
             if t + 1 == LAST and c == 0:
-                both = finished(t, c).unsqueeze(2).to_broadcast([P, U // 2, 2])
-                nc.scalar.copy(out=y_bf[c][:, :, t : t + 2], in_=both)
+                cut = U // 2 - 2
+                nc.scalar.copy(out=y_bf[c][:, :cut, t], in_=finished(t, c)[:, :cut])
+                both = finished(t, c)[:, cut:].unsqueeze(2).to_broadcast([P, 2, 2])
+                nc.scalar.copy(out=y_bf[c][:, cut:, t : t + 2], in_=both)
             else:
                 nc.scalar.copy(out=y_bf[c][:, :, t], in_=finished(t, c))
 
@@ -179,7 +182,7 @@ def tile_picked_sadam_none_po_kernel(
         nc.vector.tensor_copy(g_t[LAST][:], new_t[LAST][:].indirect(ent_t[:]))
         second_moment(0)
         first_moment(0)
-        step(0, nc.gpsimd, a_t[0])
+        step(0, a_t[0])
         for t in (2, 3):
             nc.vector.tensor_copy(a_t[t][:], m1_t[t][:].indirect(ent_t[:]))
         first_moment(1)
@@ -192,7 +195,7 @@ def tile_picked_sadam_none_po_kernel(
             if t + 2 <= LAST:
                 op = ALU.subtract if t + 2 == LAST else ALU.add
                 nc.gpsimd.tensor_tensor(moments[t + 2][:], y_3rd[t + 2][:], a_t[t + 2][:], op)
-            step(t + 1, nc.gpsimd, moments[t + 1])
+            step(t + 1, moments[t + 1])
             if t > 0:
                 y_bf.append(keep.tile([P, U // 4, PACK], BF16, name="ybf%d" % t, tag="b%d" % (t + 1), align_bytes=64))
                 for done in range(t):

@@ -24,7 +24,8 @@ SCALE_ROWS = 4
 TOP = P - QUADRANTS * SCALE_ROWS
 LIST_COLS = S // 16
 W_SPLIT = 104
-CHUNKS = (slice(0, 512), slice(512, 768), slice(768, 1024))
+STRIP = 128
+CHUNKS = (slice(1, 5), slice(0, 6, 5), slice(6, 8))
 
 
 def scale_partitions(q):
@@ -135,7 +136,7 @@ def tile_picked_sadam_none_po_kernel(
         r_t = [keep.tile([P, S], F32, name="r%d" % t) for t in range(PACK)]
         g_t = [keep.tile([P, S], F32, name="g%d" % t) for t in range(PACK)]
         u_t = [keep.tile([P, S], F32, name="u%d" % t) for t in range(PACK)]
-        y_bf = [keep.tile([P, U // 2, PACK], BF16, name="ybf0", align_bytes=64)]
+        y_bf = [keep.tile([P, 4, STRIP, PACK], BF16, name="ybf0", align_bytes=64)]
         o_c = keep.tile([P, U], U32, name="o_c", align_bytes=64)
         o_s = keep.tile([P, U], U8, name="o_s", align_bytes=64)
 
@@ -150,7 +151,10 @@ def tile_picked_sadam_none_po_kernel(
             nc.vector.tensor_tensor(a_t[t][:], m1_t[t][:].indirect(ent_t[:]), y_3rd[t][:], ALU.add)
 
         def second_moment(t):
-            nc.vector.tensor_tensor(b_t[t][:], m2_t[t][:].indirect(ent_t[:]), y_sq7[t][:], ALU.add)
+            parts = len(banks[t])
+            for h, (acc, entries) in enumerate(banks[t]):
+                part_list = ent_t[:, h * LIST_COLS // parts : (h + 1) * LIST_COLS // parts]
+                nc.vector.tensor_tensor(b_t[t][:, entries], m2_t[t][:].indirect(part_list), y_sq7[t][:, entries], ALU.add)
             nc.scalar.activation(r_t[t][:], b_t[t][:], ACT.Abs_reciprocal_sqrt, scale=0.875 / (0.5 * 0.75) ** 2)
 
         def step(t, moment):
@@ -160,16 +164,17 @@ def tile_picked_sadam_none_po_kernel(
             nc.vector.tensor_tensor(g_t[t][:], par_t[t][:].indirect(ent_t[:]), u_t[t][:], ALU.subtract)
 
         def finished(t, c):
-            return new_t[t][:, CHUNKS[c]]
+            return new_t[t][:].rearrange("p (g c) -> p g c", c=STRIP)[:, CHUNKS[c], :]
 
         def round_on_scalar(t, c):
             if t + 1 == LAST and c == 0:
-                cut = U // 2 - 2
-                nc.scalar.copy(out=y_bf[c][:, :cut, t], in_=finished(t, c)[:, :cut])
-                both = finished(t, c)[:, cut:].unsqueeze(2).to_broadcast([P, 2, 2])
-                nc.scalar.copy(out=y_bf[c][:, cut:, t : t + 2], in_=both)
+                flat = y_bf[c][:].rearrange("p g c t -> p (g c) t")
+                source = new_t[t][:, STRIP : 5 * STRIP]
+                nc.scalar.copy(out=flat[:, 2:, t], in_=source[:, 2:])
+                both = source[:, :2].unsqueeze(2).to_broadcast([P, 2, 2])
+                nc.scalar.copy(out=flat[:, :2, t : t + 2], in_=both)
             else:
-                nc.scalar.copy(out=y_bf[c][:, :, t], in_=finished(t, c))
+                nc.scalar.copy(out=y_bf[c][:, :, :, t], in_=finished(t, c))
 
         def put_back(t):
             nc.vector.tensor_copy(new_t[t][:].indirect(ent_t[:]), g_t[t][:])
@@ -197,7 +202,7 @@ def tile_picked_sadam_none_po_kernel(
                 nc.gpsimd.tensor_tensor(moments[t + 2][:], y_3rd[t + 2][:], a_t[t + 2][:], op)
             step(t + 1, moments[t + 1])
             if t > 0:
-                y_bf.append(keep.tile([P, U // 4, PACK], BF16, name="ybf%d" % t, tag="b%d" % (t + 1), align_bytes=64))
+                y_bf.append(keep.tile([P, 2, STRIP, PACK], BF16, name="ybf%d" % t, tag="b%d" % (t + 1), align_bytes=64))
                 for done in range(t):
                     round_on_scalar(done, t)
             put_back(t)
@@ -205,17 +210,33 @@ def tile_picked_sadam_none_po_kernel(
         nc.sync.dma_start(out=out_rows[:, LAST, :], in_=new_t[LAST][:])
 
         for c in (1, 2):
-            round_on_scalar(LAST, c)
-        nc.vector.tensor_copy(out=y_bf[0][:, :, LAST], in_=finished(LAST, 0))
+            for g in range(2):
+                nc.scalar.copy(out=y_bf[c][:, g, :, LAST], in_=finished(LAST, c)[:, g, :])
+        for g in (0, 2):
+            nc.vector.tensor_copy(out=y_bf[0][:, g : g + 2, :, LAST], in_=finished(LAST, 0)[:, g : g + 2, :])
         words = out_1[0].rearrange("p c r -> p (c r)").bitcast(I32)
-        for c in (1, 0, 2):
-            cols = CHUNKS[c]
+
+        def quantise(c, g, strips, first):
+            cols = slice(first * STRIP, (first + strips) * STRIP)
             nc.vector.quantize_mx(
                 out=o_c[:, cols].bitcast(FP8X4),
                 scales=o_s[:, cols],
-                in_=y_bf[c][:].rearrange("p c t -> p (c t)"),
+                in_=y_bf[c][:, g : g + strips].rearrange("p g c t -> p (g c t)"),
             )
+
+        def store_words(first, end):
+            cols = slice(first * STRIP, end * STRIP)
             nc.sync.dma_start(out=words[:, cols], in_=o_c[:, cols].bitcast(I32))
+
+        quantise(0, 0, 2, 1)
+        quantise(1, 0, 1, 0)
+        store_words(0, 3)
+        quantise(1, 1, 1, 5)
+        quantise(0, 2, 2, 3)
+        store_words(3, 6)
+        quantise(2, 0, 1, 6)
+        quantise(2, 1, 1, 7)
+        store_words(6, 8)
         for q in range(QUADRANTS):
             queue = nc.scalar if q % 2 == 0 else nc.sync
             queue.dma_start(out=out_2[0, scale_rows(q), :].bitcast(I32), in_=o_s[scale_partitions(q), :].bitcast(I32))

@@ -56,7 +56,7 @@ def tile_picked_sadam_none_po_kernel(
         with tc.tile_pool(name="head", bufs=1) as head:
             xs = head.tile([P, T], U8, name="xs")
             nc.sync.dma_start(offs_t[:], offs)
-            nc.sync.dma_start(out=xs[TOP:, :].bitcast(I32), in_=x_scales[0].bitcast(I32))
+            nc.scalar.dma_start(out=xs[TOP:, :].bitcast(I32), in_=x_scales[0].bitcast(I32))
             nc.sync.dma_start(out=w_raw[:], in_=w1.rearrange("(p j) c -> p j c", j=PACK))
             nc.sync.dma_start(out=xw[:], in_=x_words[0].rearrange("p c r -> p (c r)").bitcast(I32))
             nc.sync.dma_start(ent_t[:], ent)
@@ -82,16 +82,15 @@ def tile_picked_sadam_none_po_kernel(
         def load(tiles, rows, t):
             nc.sync.dma_start(out=tiles[t][:], in_=rows[:, t, :])
 
-        load(new_t, par_rows, LAST)
-        load(m2_t, m2_rows, 0)
-        load(m1_t, m1_rows, 0)
-        load(m1_t, m1_rows, 2)
-        load(m1_t, m1_rows, 3)
-        load(m1_t, m1_rows, 1)
-        for t in range(LAST):
-            load(par_t, par_rows, t)
-            load(m2_t, m2_rows, t + 1)
-            load(new_t, par_rows, t)
+        for t in range(PACK):
+            if t == LAST:
+                load(new_t, par_rows, t)
+            load(m2_t, m2_rows, t)
+            load(m1_t, m1_rows, t)
+            if t < LAST:
+                load(par_t, par_rows, t)
+            if t > 0:
+                load(new_t, par_rows, t - 1)
 
         w_bf = keep.tile([P, PACK * P * PACK], BF16, name="w_bf", align_bytes=64)
         w_dst = w_bf[:].rearrange("p (t m j) -> p m j t", t=PACK, j=PACK)
@@ -131,12 +130,18 @@ def tile_picked_sadam_none_po_kernel(
                 plane_banks.append((acc, entries))
             banks.append(plane_banks)
 
+        m2_g = [keep.tile([P, S], F32, name="m2g%d" % t) for t in range(PACK)]
+        m1_g = [keep.tile([P, S], F32, name="m1g%d" % t) for t in range(PACK)]
+        par_g = [keep.tile([P, S], F32, name="parg%d" % t) for t in range(PACK)]
+        b_t = [keep.tile([P, S], F32, name="b%d" % t) for t in range(PACK)]
         a_t = [keep.tile([P, S], F32, name="a%d" % t) for t in range(PACK)]
-        b_t = [keep.tile([P, S], F32, name="b%d" % t, align_bytes=64) for t in range(PACK)]
         r_t = [keep.tile([P, S], F32, name="r%d" % t) for t in range(PACK)]
-        g_t = [keep.tile([P, S], F32, name="g%d" % t) for t in range(PACK)]
         u_t = [keep.tile([P, S], F32, name="u%d" % t) for t in range(PACK)]
-        y_bf = [keep.tile([P, 4, STRIP, PACK], BF16, name="ybf0", align_bytes=64)]
+        g_t = [keep.tile([P, S], F32, name="g%d" % t) for t in range(LAST)]
+        y_bf = [
+            keep.tile([P, strips, STRIP, PACK], BF16, name="ybf%d" % c, align_bytes=64)
+            for c, strips in enumerate((4, 2, 2))
+        ]
         o_c = keep.tile([P, U], U32, name="o_c", align_bytes=64)
         o_s = keep.tile([P, U], U8, name="o_s", align_bytes=64)
 
@@ -147,66 +152,42 @@ def tile_picked_sadam_none_po_kernel(
             for acc, entries in banks[t]:
                 nc.scalar.activation(y_3rd[t][:, entries], acc[:], ACT.Copy, scale=sign * 0.25 / 0.75)
 
-        def first_moment(t):
-            nc.vector.tensor_tensor(a_t[t][:], m1_t[t][:].indirect(ent_t[:]), y_3rd[t][:], ALU.add)
-
-        def second_moment(t):
-            parts = len(banks[t])
-            for h, (acc, entries) in enumerate(banks[t]):
-                part_list = ent_t[:, h * LIST_COLS // parts : (h + 1) * LIST_COLS // parts]
-                nc.vector.tensor_tensor(b_t[t][:, entries], m2_t[t][:].indirect(part_list), y_sq7[t][:, entries], ALU.add)
-            nc.scalar.activation(r_t[t][:], b_t[t][:], ACT.Abs_reciprocal_sqrt, scale=0.875 / (0.5 * 0.75) ** 2)
-
-        def step(t, moment):
-            nc.gpsimd.tensor_tensor(u_t[t][:], moment[:], r_t[t][:], ALU.mult)
-
-        def new_par(t):
-            nc.vector.tensor_tensor(g_t[t][:], par_t[t][:].indirect(ent_t[:]), u_t[t][:], ALU.subtract)
+        def fetch(picked, table):
+            nc.vector.tensor_copy(picked, table[:].indirect(ent_t[:]))
 
         def finished(t, c):
             return new_t[t][:].rearrange("p (g c) -> p g c", c=STRIP)[:, CHUNKS[c], :]
 
         def round_on_scalar(t, c):
             if t + 1 == LAST and c == 0:
-                flat = y_bf[c][:].rearrange("p g c t -> p (g c) t")
-                source = new_t[t][:, STRIP : 5 * STRIP]
-                nc.scalar.copy(out=flat[:, 2:, t], in_=source[:, 2:])
-                both = source[:, :2].unsqueeze(2).to_broadcast([P, 2, 2])
-                nc.scalar.copy(out=flat[:, :2, t : t + 2], in_=both)
+                rounded = y_bf[c][:].rearrange("p (h g) c t -> p h (g c) t", h=2)
+                source = new_t[t][:, STRIP : 5 * STRIP].rearrange("p (h c) -> p h c", h=2)
+                nc.scalar.copy(out=rounded[:, :, 2:, t], in_=source[:, :, 2:])
+                both = source[:, :, :2].unsqueeze(3).to_broadcast([P, 2, 2, 2])
+                nc.scalar.copy(out=rounded[:, :, :2, t : t + 2], in_=both)
             else:
                 nc.scalar.copy(out=y_bf[c][:, :, :, t], in_=finished(t, c))
 
-        def put_back(t):
-            nc.vector.tensor_copy(new_t[t][:].indirect(ent_t[:]), g_t[t][:])
-            nc.sync.dma_start(out=out_rows[:, t, :], in_=new_t[t][:])
-            for c in range(len(y_bf)):
-                round_on_scalar(t, c)
-
-        leave_bank(0)
-        leave_bank(1)
-        nc.vector.tensor_copy(g_t[LAST][:], new_t[LAST][:].indirect(ent_t[:]))
-        second_moment(0)
-        first_moment(0)
-        step(0, a_t[0])
-        for t in (2, 3):
-            nc.vector.tensor_copy(a_t[t][:], m1_t[t][:].indirect(ent_t[:]))
-        first_moment(1)
-        leave_bank(2)
-        leave_bank(3)
-        moments = [a_t[0], a_t[1], y_sq7[1], y_sq7[2]]
-        for t in range(LAST):
-            new_par(t)
-            second_moment(t + 1)
-            if t + 2 <= LAST:
-                op = ALU.subtract if t + 2 == LAST else ALU.add
-                nc.gpsimd.tensor_tensor(moments[t + 2][:], y_3rd[t + 2][:], a_t[t + 2][:], op)
-            step(t + 1, moments[t + 1])
-            if t > 0:
-                y_bf.append(keep.tile([P, 2, STRIP, PACK], BF16, name="ybf%d" % t, tag="b%d" % (t + 1), align_bytes=64))
-                for done in range(t):
-                    round_on_scalar(done, t)
-            put_back(t)
-        nc.vector.tensor_tensor(new_t[LAST][:].indirect(ent_t[:]), g_t[LAST][:], u_t[LAST][:], ALU.add)
+        for t in range(PACK):
+            leave_bank(t)
+            if t == LAST:
+                fetch(par_g[t][:], new_t[t])
+            fetch(m2_g[t][:], m2_t[t])
+            fetch(m1_g[t][:], m1_t[t])
+            if t < LAST:
+                fetch(par_g[t][:], par_t[t])
+            nc.gpsimd.tensor_tensor(b_t[t][:], y_sq7[t][:], m2_g[t][:], ALU.add)
+            nc.scalar.activation(r_t[t][:], b_t[t][:], ACT.Abs_reciprocal_sqrt, scale=0.875 / (0.5 * 0.75) ** 2)
+            nc.gpsimd.tensor_tensor(a_t[t][:], y_3rd[t][:], m1_g[t][:], ALU.subtract if t == LAST else ALU.add)
+            nc.gpsimd.tensor_tensor(u_t[t][:], a_t[t][:], r_t[t][:], ALU.mult)
+            if t < LAST:
+                nc.gpsimd.tensor_tensor(g_t[t][:], par_g[t][:], u_t[t][:], ALU.subtract)
+            for done in range(max(t - 1, 0), t):
+                nc.vector.tensor_copy(new_t[done][:].indirect(ent_t[:]), g_t[done][:])
+                nc.sync.dma_start(out=out_rows[:, done, :], in_=new_t[done][:])
+                for c in range(3):
+                    round_on_scalar(done, c)
+        nc.vector.tensor_tensor(new_t[LAST][:].indirect(ent_t[:]), par_g[LAST][:], u_t[LAST][:], ALU.add)
         nc.sync.dma_start(out=out_rows[:, LAST, :], in_=new_t[LAST][:])
 
         for c in (1, 2):

@@ -24,8 +24,8 @@ SCALE_ROWS = 4
 TOP = P - QUADRANTS * SCALE_ROWS
 LIST_COLS = S // 16
 W_SPLIT = 104
-STRIP = 128
-CHUNKS = (slice(1, 5), slice(0, 6, 5), slice(6, 8))
+CHUNK = 256
+PLACE = 4 * S
 
 
 def scale_partitions(q):
@@ -69,11 +69,14 @@ def tile_picked_sadam_none_po_kernel(
             picked = slice(TOP + SCALE_ROWS * q, TOP + SCALE_ROWS * (q + 1))
             nc.sync.dma_start(out=xq_s[scale_partitions(q), :].bitcast(I32), in_=xg_s[picked, :].bitcast(I32))
 
-        tables = ctx.enter_context(tc.tile_pool(name="tables", bufs=1))
-        par_t = [tables.tile([P, U], F32, name="par%d" % t) for t in range(LAST)]
-        new_t = [tables.tile([P, U], F32, name="new%d" % t) for t in range(PACK)]
-        m1_t = [tables.tile([P, U], F32, name="m1_%d" % t) for t in range(PACK)]
-        m2_t = [tables.tile([P, U], F32, name="m2_%d" % t) for t in range(PACK)]
+        work = ctx.enter_context(tc.tile_pool(name="work", bufs=1))
+
+        def placed(name, shape, dtype, place):
+            return work.tile(shape, dtype, name=name, offset=int(place * PLACE), align_bytes=64)
+
+        new_t = [placed("new%d" % t, [P, U], F32, 20 + 2 * t) for t in range(PACK)]
+        m1_t = [placed("m1_%d" % t, [P, U], F32, 28 + 2 * t) for t in range(PACK)]
+        m2_t = [placed("m2_%d" % t, [P, U], F32, at) for t, at in enumerate((36, 42, 38, 40))]
         par_rows = par.rearrange("(p t) u -> p t u", t=PACK)
         m1_rows = m1.rearrange("(p t) u -> p t u", t=PACK)
         m2_rows = m2.rearrange("(p t) u -> p t u", t=PACK)
@@ -82,24 +85,34 @@ def tile_picked_sadam_none_po_kernel(
         def load(tiles, rows, t):
             nc.sync.dma_start(out=tiles[t][:], in_=rows[:, t, :])
 
-        for t in range(PACK):
-            if t == LAST:
-                load(new_t, par_rows, t)
-            load(m2_t, m2_rows, t)
-            load(m1_t, m1_rows, t)
-            if t < LAST:
-                load(par_t, par_rows, t)
-            if t > 0:
-                load(new_t, par_rows, t - 1)
+        for tiles, rows, t in (
+            (m2_t, m2_rows, 0),
+            (m1_t, m1_rows, 0),
+            (m2_t, m2_rows, 1),
+            (m1_t, m1_rows, 1),
+            (new_t, par_rows, 0),
+            (m2_t, m2_rows, 2),
+            (m1_t, m1_rows, 2),
+            (new_t, par_rows, 1),
+            (m1_t, m1_rows, 3),
+            (new_t, par_rows, 2),
+            (new_t, par_rows, 3),
+            (m2_t, m2_rows, 3),
+        ):
+            load(tiles, rows, t)
 
         w_bf = keep.tile([P, PACK * P * PACK], BF16, name="w_bf", align_bytes=64)
         w_dst = w_bf[:].rearrange("p (t m j) -> p m j t", t=PACK, j=PACK)
         w_src = w_raw[:].rearrange("p j (m t) -> p m j t", t=PACK)
         nc.vector.tensor_copy(out=w_dst[:, :W_SPLIT], in_=w_src[:, :W_SPLIT])
         nc.scalar.copy(out=w_dst[:, W_SPLIT:], in_=w_src[:, W_SPLIT:])
-        w_c = keep.tile([P, N], U32, name="w_c", align_bytes=64)
+        w_c = [placed("w_c0", [P, N // 2], U32, 0), keep.tile([P, N // 2], U32, name="w_c1", align_bytes=64)]
         w_s = keep.tile([P, N], U8, name="w_s", align_bytes=64)
-        nc.vector.quantize_mx(out=w_c[:].bitcast(FP8X4), scales=w_s[:], in_=w_bf[:])
+        for h in range(2):
+            half = slice(h * N // 2, (h + 1) * N // 2)
+            nc.vector.quantize_mx(
+                out=w_c[h][:].bitcast(FP8X4), scales=w_s[:, half], in_=w_bf[:, h * 2 * N : (h + 1) * 2 * N]
+            )
 
         xq_c = keep.tile([P, S], U32, name="xq_c", align_bytes=64)
         for h in range(2):
@@ -107,8 +120,6 @@ def tile_picked_sadam_none_po_kernel(
             half_list = slice(h * LIST_COLS // 2, (h + 1) * LIST_COLS // 2)
             nc.vector.tensor_copy(xq_c[:, half], xw[:].bitcast(U32).indirect(offs_t[:, half_list]))
 
-        y_sq7 = [keep.tile([P, S], F32, name="ysq%d" % t) for t in range(PACK)]
-        y_3rd = [keep.tile([P, S], F32, name="yth%d" % t) for t in range(PACK)]
         banks = []
         for t in range(PACK):
             features = slice(t * P, (t + 1) * P)
@@ -120,7 +131,7 @@ def tile_picked_sadam_none_po_kernel(
                 entries = slice(h * width, (h + 1) * width)
                 nc.tensor.matmul_mx(
                     out=acc[:],
-                    lhsT=w_c[:, features].bitcast(FP8X4),
+                    lhsT=w_c[t // 2][:, t % 2 * P : (t % 2 + 1) * P].bitcast(FP8X4),
                     lhsT_scale=w_s[:, features],
                     rhs=xq_c[:, entries].bitcast(FP8X4),
                     rhs_scale=xq_s[:, entries],
@@ -130,94 +141,132 @@ def tile_picked_sadam_none_po_kernel(
                 plane_banks.append((acc, entries))
             banks.append(plane_banks)
 
-        m2_g = [keep.tile([P, S], F32, name="m2g%d" % t) for t in range(PACK)]
-        m1_g = [keep.tile([P, S], F32, name="m1g%d" % t) for t in range(PACK)]
-        par_g = [keep.tile([P, S], F32, name="parg%d" % t) for t in range(PACK)]
-        b_t = [keep.tile([P, S], F32, name="b%d" % t) for t in range(PACK)]
-        a_t = [keep.tile([P, S], F32, name="a%d" % t) for t in range(PACK)]
-        r_t = [keep.tile([P, S], F32, name="r%d" % t) for t in range(PACK)]
+        def picked(name, places):
+            return {t: placed(name + str(t), [P, S], F32, at) for t, at in places}
+
+        m1_g = picked("m1g", ((0, 0), (1, 1), (2, 2), (3, 5)))
+        m2_g = picked("m2g", ((0, 1), (2, 7), (3, 12.5)))
+        y_sq7 = picked("ysq", ((0, 6), (1, 8), (2, 31), (3, 34)))
+        r_t = picked("r", ((0, 28), (1, 30), (2, 35), (3, 44)))
+        b_t = picked("b", ((0, 3), (1, 4), (2, 15), (3, 6)))
+        par_g = picked("parg", ((1, 10), (2, 16), (3, 40)))
+        a_t = picked("a", ((0, 8), (1, 18), (2, 19), (3, 10)))
         u_t = [keep.tile([P, S], F32, name="u%d" % t) for t in range(PACK)]
         g_t = [keep.tile([P, S], F32, name="g%d" % t) for t in range(LAST)]
-        y_bf = [
-            keep.tile([P, strips, STRIP, PACK], BF16, name="ybf%d" % c, align_bytes=64)
-            for c, strips in enumerate((4, 2, 2))
-        ]
+        pairs = [placed("pairs%d" % s, [P, 2, U // 2, 2], BF16, 11 + 2 * s) for s in range(2)]
+        y_bf = [keep.tile([P, CHUNK * PACK], BF16, name="ybf%d" % c, align_bytes=64) for c in range(4)]
         o_c = keep.tile([P, U], U32, name="o_c", align_bytes=64)
         o_s = keep.tile([P, U], U8, name="o_s", align_bytes=64)
 
-        def leave_bank(t):
-            sign = -1.0 if t == LAST else 1.0
+        def square(t):
             for acc, entries in banks[t]:
                 nc.scalar.activation(y_sq7[t][:, entries], acc[:], ACT.Square, scale=root[:])
+
+        def first_moment(t):
+            sign, op = (-1.0, ALU.subtract) if t == LAST else (1.0, ALU.add)
             for acc, entries in banks[t]:
-                nc.scalar.activation(y_3rd[t][:, entries], acc[:], ACT.Copy, scale=sign * 0.25 / 0.75)
+                nc.vector.scalar_tensor_tensor(
+                    a_t[t][:, entries], acc[:], sign * 0.25 / 0.75, m1_g[t][:, entries], ALU.mult, op
+                )
 
-        def fetch(picked, table):
-            nc.vector.tensor_copy(picked, table[:].indirect(ent_t[:]))
-
-        def finished(t, c):
-            return new_t[t][:].rearrange("p (g c) -> p g c", c=STRIP)[:, CHUNKS[c], :]
-
-        def round_on_scalar(t, c):
-            if t + 1 == LAST and c == 0:
-                rounded = y_bf[c][:].rearrange("p (h g) c t -> p h (g c) t", h=2)
-                source = new_t[t][:, STRIP : 5 * STRIP].rearrange("p (h c) -> p h c", h=2)
-                nc.scalar.copy(out=rounded[:, :, 2:, t], in_=source[:, :, 2:])
-                both = source[:, :, :2].unsqueeze(3).to_broadcast([P, 2, 2, 2])
-                nc.scalar.copy(out=rounded[:, :, :2, t : t + 2], in_=both)
-            else:
-                nc.scalar.copy(out=y_bf[c][:, :, :, t], in_=finished(t, c))
-
-        for t in range(PACK):
-            leave_bank(t)
-            if t == LAST:
-                fetch(par_g[t][:], new_t[t])
-            fetch(m2_g[t][:], m2_t[t])
-            fetch(m1_g[t][:], m1_t[t])
-            if t < LAST:
-                fetch(par_g[t][:], par_t[t])
-            nc.gpsimd.tensor_tensor(b_t[t][:], y_sq7[t][:], m2_g[t][:], ALU.add)
+        def inverse_root(t):
             nc.scalar.activation(r_t[t][:], b_t[t][:], ACT.Abs_reciprocal_sqrt, scale=0.875 / (0.5 * 0.75) ** 2)
-            nc.gpsimd.tensor_tensor(a_t[t][:], y_3rd[t][:], m1_g[t][:], ALU.subtract if t == LAST else ALU.add)
+
+        def fetch_on_vector(picked, table):
+            nc.vector.tensor_copy(picked[:], table[:].indirect(ent_t[:]))
+
+        def fetch_on_scalar(picked, table):
+            nc.scalar.activation(picked[:], table[:].indirect(ent_t[:]), ACT.Copy)
+
+        def put_back(t):
+            nc.vector.tensor_copy(new_t[t][:].indirect(ent_t[:]), g_t[t][:])
+            nc.sync.dma_start(out=out_rows[:, t, :], in_=new_t[t][:])
+
+        def second_moment(t):
+            nc.gpsimd.tensor_tensor(b_t[t][:], y_sq7[t][:], m2_g[t][:], ALU.add)
+
+        def step(t):
             nc.gpsimd.tensor_tensor(u_t[t][:], a_t[t][:], r_t[t][:], ALU.mult)
-            if t < LAST:
-                nc.gpsimd.tensor_tensor(g_t[t][:], par_g[t][:], u_t[t][:], ALU.subtract)
-            for done in range(max(t - 1, 0), t):
-                nc.vector.tensor_copy(new_t[done][:].indirect(ent_t[:]), g_t[done][:])
-                nc.sync.dma_start(out=out_rows[:, done, :], in_=new_t[done][:])
-                for c in range(3):
-                    round_on_scalar(done, c)
+
+        def take_step(t):
+            nc.gpsimd.tensor_tensor(g_t[t][:], par_g[t][:], u_t[t][:], ALU.subtract)
+
+        square(0)
+        square(1)
+        fetch_on_vector(m2_g[0], m2_t[0])
+        fetch_on_scalar(m1_g[0], m1_t[0])
+        nc.vector.tensor_tensor(b_t[0][:], y_sq7[0][:], m2_g[0][:], ALU.add)
+        nc.vector.tensor_tensor(b_t[1][:], m2_t[1][:].indirect(ent_t[:]), y_sq7[1][:], ALU.add)
+        inverse_root(0)
+        first_moment(0)
+        nc.vector.tensor_tensor(u_t[0][:], a_t[0][:], r_t[0][:], ALU.mult)
+        fetch_on_scalar(m1_g[1], m1_t[1])
+        inverse_root(1)
+        first_moment(1)
+        nc.vector.tensor_tensor(g_t[0][:], new_t[0][:].indirect(ent_t[:]), u_t[0][:], ALU.subtract)
+        put_back(0)
+        step(1)
+        square(2)
+        fetch_on_scalar(m2_g[2], m2_t[2])
+        second_moment(2)
+        fetch_on_scalar(m1_g[2], m1_t[2])
+        first_moment(2)
+        fetch_on_scalar(par_g[1], new_t[1])
+        take_step(1)
+        put_back(1)
+        fetch_on_scalar(m1_g[3], m1_t[3])
+        inverse_root(2)
+        step(2)
+        square(3)
+        first_moment(3)
+        fetch_on_scalar(par_g[2], new_t[2])
+        take_step(2)
+        put_back(2)
+        fetch_on_scalar(m2_g[3], m2_t[3])
+        second_moment(3)
+        fetch_on_scalar(par_g[3], new_t[3])
+        inverse_root(3)
+        step(3)
         nc.vector.tensor_tensor(new_t[LAST][:].indirect(ent_t[:]), par_g[LAST][:], u_t[LAST][:], ALU.add)
         nc.sync.dma_start(out=out_rows[:, LAST, :], in_=new_t[LAST][:])
 
-        for c in (1, 2):
-            for g in range(2):
-                nc.scalar.copy(out=y_bf[c][:, g, :, LAST], in_=finished(LAST, c)[:, g, :])
-        for g in (0, 2):
-            nc.vector.tensor_copy(out=y_bf[0][:, g : g + 2, :, LAST], in_=finished(LAST, 0)[:, g : g + 2, :])
+        def columns(t, s):
+            return new_t[t][:, s * U // 2 : (s + 1) * U // 2]
+
+        for t in range(2):
+            for s in range(2):
+                nc.scalar.copy(out=pairs[s][:, 0, :, t], in_=columns(t, s))
+        rounded = pairs[0][:, 1].rearrange("p (h c) e -> p h c e", h=2)
+        source = columns(2, 0).rearrange("p (h c) -> p h c", h=2)
+        nc.scalar.copy(out=rounded[:, :, 2:, 0], in_=source[:, :, 2:])
+        nc.scalar.copy(out=rounded[:, :, :2, :], in_=source[:, :, :2].unsqueeze(3).to_broadcast([P, 2, 2, 2]))
+        nc.scalar.copy(out=pairs[1][:, 1, :, 0], in_=columns(2, 1))
+
+        def chunk(c):
+            return slice(c % 2 * CHUNK, (c % 2 + 1) * CHUNK)
+
+        def round_last(c, copy):
+            copy(out=pairs[c // 2][:, 1, chunk(c), 1], in_=columns(LAST, c // 2)[:, chunk(c)])
+
+        def weave(c, copy, word):
+            both = pairs[c // 2][:].bitcast(word).rearrange("p h c e -> p c (h e)")
+            copy(out=y_bf[c][:].bitcast(word).rearrange("p (c h) -> p c h", h=2), in_=both[:, chunk(c), :])
+
         words = out_1[0].rearrange("p c r -> p (c r)").bitcast(I32)
 
-        def quantise(c, g, strips, first):
-            cols = slice(first * STRIP, (first + strips) * STRIP)
-            nc.vector.quantize_mx(
-                out=o_c[:, cols].bitcast(FP8X4),
-                scales=o_s[:, cols],
-                in_=y_bf[c][:, g : g + strips].rearrange("p g c t -> p (g c t)"),
-            )
-
-        def store_words(first, end):
-            cols = slice(first * STRIP, end * STRIP)
+        def quantise(c):
+            cols = slice(c * CHUNK, (c + 1) * CHUNK)
+            nc.vector.quantize_mx(out=o_c[:, cols].bitcast(FP8X4), scales=o_s[:, cols], in_=y_bf[c][:])
             nc.sync.dma_start(out=words[:, cols], in_=o_c[:, cols].bitcast(I32))
 
-        quantise(0, 0, 2, 1)
-        quantise(1, 0, 1, 0)
-        store_words(0, 3)
-        quantise(1, 1, 1, 5)
-        quantise(0, 2, 2, 3)
-        store_words(3, 6)
-        quantise(2, 0, 1, 6)
-        quantise(2, 1, 1, 7)
-        store_words(6, 8)
+        for c in range(2):
+            round_last(c, nc.vector.tensor_copy)
+            round_last(c + 2, nc.scalar.copy)
+        for c in range(2):
+            weave(c, nc.vector.tensor_copy, I32)
+            weave(c + 2, nc.scalar.copy, U32)
+        for c in range(4):
+            quantise(c)
         for q in range(QUADRANTS):
             queue = nc.scalar if q % 2 == 0 else nc.sync
             queue.dma_start(out=out_2[0, scale_rows(q), :].bitcast(I32), in_=o_s[scale_partitions(q), :].bitcast(I32))

@@ -75,7 +75,7 @@ def tile_picked_sadam_none_po_kernel(
             return work.tile(shape, dtype, name=name, offset=int(place * PLACE), align_bytes=64)
 
         new_t = [placed("new%d" % t, [P, U], F32, 20 + 2 * t) for t in range(PACK)]
-        m1_t = [placed("m1_%d" % t, [P, U], F32, 28 + 2 * t) for t in range(PACK)]
+        m1_t = [placed("m1_%d" % t, [P, U], F32, at) for t, at in enumerate((49, 30, 32, 34))]
         m2_t = [placed("m2_%d" % t, [P, U], F32, at) for t, at in enumerate((36, 42, 38, 40))]
         par_rows = par.rearrange("(p t) u -> p t u", t=PACK)
         m1_rows = m1.rearrange("(p t) u -> p t u", t=PACK)
@@ -106,13 +106,9 @@ def tile_picked_sadam_none_po_kernel(
         w_src = w_raw[:].rearrange("p j (m t) -> p m j t", t=PACK)
         nc.vector.tensor_copy(out=w_dst[:, :W_SPLIT], in_=w_src[:, :W_SPLIT])
         nc.scalar.copy(out=w_dst[:, W_SPLIT:], in_=w_src[:, W_SPLIT:])
-        w_c = [placed("w_c0", [P, N // 2], U32, 0), keep.tile([P, N // 2], U32, name="w_c1", align_bytes=64)]
+        w_c = placed("w_c", [P, N], U32, 0)
         w_s = keep.tile([P, N], U8, name="w_s", align_bytes=64)
-        for h in range(2):
-            half = slice(h * N // 2, (h + 1) * N // 2)
-            nc.vector.quantize_mx(
-                out=w_c[h][:].bitcast(FP8X4), scales=w_s[:, half], in_=w_bf[:, h * 2 * N : (h + 1) * 2 * N]
-            )
+        nc.vector.quantize_mx(out=w_c[:].bitcast(FP8X4), scales=w_s[:], in_=w_bf[:])
 
         xq_c = keep.tile([P, S], U32, name="xq_c", align_bytes=64)
         for h in range(2):
@@ -131,7 +127,7 @@ def tile_picked_sadam_none_po_kernel(
                 entries = slice(h * width, (h + 1) * width)
                 nc.tensor.matmul_mx(
                     out=acc[:],
-                    lhsT=w_c[t // 2][:, t % 2 * P : (t % 2 + 1) * P].bitcast(FP8X4),
+                    lhsT=w_c[:, features].bitcast(FP8X4),
                     lhsT_scale=w_s[:, features],
                     rhs=xq_c[:, entries].bitcast(FP8X4),
                     rhs_scale=xq_s[:, entries],
@@ -144,14 +140,14 @@ def tile_picked_sadam_none_po_kernel(
         def picked(name, places):
             return {t: placed(name + str(t), [P, S], F32, at) for t, at in places}
 
-        m1_g = picked("m1g", ((0, 0), (1, 1), (2, 2), (3, 5)))
-        m2_g = picked("m2g", ((0, 1), (2, 7), (3, 12.5)))
-        y_sq7 = picked("ysq", ((0, 6), (1, 8), (2, 31), (3, 34)))
-        r_t = picked("r", ((0, 28), (1, 30), (2, 35), (3, 44)))
+        m1_g = picked("m1g", ((0, 1), (1, 7), (2, 2), (3, 5)))
+        m2_g = picked("m2g", ((0, 9), (2, 17), (3, 12.5)))
+        y_sq7 = picked("ysq", ((0, 6), (1, 8), (2, 28), (3, 29)))
+        r_t = picked("r", ((0, 0), (1, 30), (2, 35), (3, 44)))
         b_t = picked("b", ((0, 3), (1, 4), (2, 15), (3, 6)))
         par_g = picked("parg", ((1, 10), (2, 16), (3, 40)))
-        a_t = picked("a", ((0, 8), (1, 18), (2, 19), (3, 10)))
-        u_t = [keep.tile([P, S], F32, name="u%d" % t) for t in range(PACK)]
+        a_t = picked("a", ((0, 45), (1, 18), (2, 19), (3, 10)))
+        u_t = picked("u", ((0, 8), (1, 46), (2, 47), (3, 48)))
         g_t = [keep.tile([P, S], F32, name="g%d" % t) for t in range(LAST)]
         pairs = [placed("pairs%d" % s, [P, 2, U // 2, 2], BF16, 11 + 2 * s) for s in range(2)]
         y_bf = [keep.tile([P, CHUNK * PACK], BF16, name="ybf%d" % c, align_bytes=64) for c in range(4)]
@@ -191,14 +187,14 @@ def tile_picked_sadam_none_po_kernel(
         def take_step(t):
             nc.gpsimd.tensor_tensor(g_t[t][:], par_g[t][:], u_t[t][:], ALU.subtract)
 
-        square(0)
-        square(1)
+        for t in range(PACK):
+            square(t)
         fetch_on_vector(m2_g[0], m2_t[0])
-        fetch_on_scalar(m1_g[0], m1_t[0])
-        nc.vector.tensor_tensor(b_t[0][:], y_sq7[0][:], m2_g[0][:], ALU.add)
-        nc.vector.tensor_tensor(b_t[1][:], m2_t[1][:].indirect(ent_t[:]), y_sq7[1][:], ALU.add)
+        fetch_on_vector(m1_g[0], m1_t[0])
+        second_moment(0)
         inverse_root(0)
         first_moment(0)
+        nc.vector.tensor_tensor(b_t[1][:], m2_t[1][:].indirect(ent_t[:]), y_sq7[1][:], ALU.add)
         nc.vector.tensor_tensor(u_t[0][:], a_t[0][:], r_t[0][:], ALU.mult)
         fetch_on_scalar(m1_g[1], m1_t[1])
         inverse_root(1)
@@ -206,7 +202,6 @@ def tile_picked_sadam_none_po_kernel(
         nc.vector.tensor_tensor(g_t[0][:], new_t[0][:].indirect(ent_t[:]), u_t[0][:], ALU.subtract)
         put_back(0)
         step(1)
-        square(2)
         fetch_on_scalar(m2_g[2], m2_t[2])
         second_moment(2)
         fetch_on_scalar(m1_g[2], m1_t[2])
@@ -217,7 +212,6 @@ def tile_picked_sadam_none_po_kernel(
         fetch_on_scalar(m1_g[3], m1_t[3])
         inverse_root(2)
         step(2)
-        square(3)
         first_moment(3)
         fetch_on_scalar(par_g[2], new_t[2])
         take_step(2)

@@ -87,8 +87,8 @@ def tile_picked_sadam_none_po_kernel(
 
         for tiles, rows, t in (
             (m2_t, m2_rows, 0),
-            (m1_t, m1_rows, 0),
             (m2_t, m2_rows, 1),
+            (m1_t, m1_rows, 0),
             (m1_t, m1_rows, 1),
             (new_t, par_rows, 0),
             (m2_t, m2_rows, 2),
@@ -141,13 +141,13 @@ def tile_picked_sadam_none_po_kernel(
             return {t: placed(name + str(t), [P, S], F32, at) for t, at in places}
 
         m1_g = picked("m1g", ((0, 1), (1, 7), (2, 2), (3, 5)))
-        m2_g = picked("m2g", ((0, 9), (2, 17), (3, 12.5)))
+        m2_g = picked("m2g", ((0, 9), (1, 51), (2, 17), (3, 12.5)))
         y_sq7 = picked("ysq", ((0, 6), (1, 8), (2, 28), (3, 29)))
         r_t = picked("r", ((0, 0), (1, 30), (2, 35), (3, 44)))
         b_t = picked("b", ((0, 3), (1, 4), (2, 15), (3, 6)))
         par_g = picked("parg", ((1, 10), (2, 16), (3, 40)))
         a_t = picked("a", ((0, 45), (1, 18), (2, 19), (3, 10)))
-        u_t = picked("u", ((0, 8), (1, 46), (2, 47), (3, 48)))
+        u_t = picked("u", ((0, 52), (1, 46), (2, 47), (3, 48)))
         g_t = [keep.tile([P, S], F32, name="g%d" % t) for t in range(LAST)]
         pairs = [placed("pairs%d" % s, [P, 2, U // 2, 2], BF16, 11 + 2 * s) for s in range(2)]
         y_bf = [keep.tile([P, CHUNK * PACK], BF16, name="ybf%d" % c, align_bytes=64) for c in range(4)]
@@ -190,11 +190,12 @@ def tile_picked_sadam_none_po_kernel(
         for t in range(PACK):
             square(t)
         fetch_on_vector(m2_g[0], m2_t[0])
-        fetch_on_vector(m1_g[0], m1_t[0])
         second_moment(0)
+        fetch_on_vector(m2_g[1], m2_t[1])
+        second_moment(1)
+        fetch_on_vector(m1_g[0], m1_t[0])
         inverse_root(0)
         first_moment(0)
-        nc.vector.tensor_tensor(b_t[1][:], m2_t[1][:].indirect(ent_t[:]), y_sq7[1][:], ALU.add)
         nc.vector.tensor_tensor(u_t[0][:], a_t[0][:], r_t[0][:], ALU.mult)
         fetch_on_scalar(m1_g[1], m1_t[1])
         inverse_root(1)

@@ -178,6 +178,9 @@ def tile_picked_sadam_none_po_kernel(
             nc.vector.tensor_copy(new_t[t][:].indirect(ent_t[:]), g_t[t][:])
             nc.sync.dma_start(out=out_rows[:, t, :], in_=new_t[t][:])
 
+        halves = [slice(h * S // 2, (h + 1) * S // 2) for h in range(2)]
+        half_lists = [slice(h * LIST_COLS // 2, (h + 1) * LIST_COLS // 2) for h in range(2)]
+
         def second_moment(t):
             nc.gpsimd.tensor_tensor(b_t[t][:], y_sq7[t][:], m2_g[t][:], ALU.add)
 
@@ -193,10 +196,12 @@ def tile_picked_sadam_none_po_kernel(
         second_moment(0)
         fetch_on_vector(m2_g[1], m2_t[1])
         second_moment(1)
-        fetch_on_vector(m1_g[0], m1_t[0])
+        for h in range(2):
+            nc.vector.tensor_copy(m1_g[0][:, halves[h]], m1_t[0][:].indirect(ent_t[:, half_lists[h]]))
         inverse_root(0)
         first_moment(0)
-        nc.vector.tensor_tensor(u_t[0][:], a_t[0][:], r_t[0][:], ALU.mult)
+        for half in halves:
+            nc.vector.tensor_tensor(u_t[0][:, half], a_t[0][:, half], r_t[0][:, half], ALU.mult)
         fetch_on_scalar(m1_g[1], m1_t[1])
         inverse_root(1)
         first_moment(1)

@@ -152,7 +152,7 @@ def tile_picked_sadam_none_po_kernel(
         pairs = [placed("pairs%d" % s, [P, 2, U // 2, 2], BF16, 11 + 2 * s) for s in range(2)]
         y_bf = [keep.tile([P, CHUNK * PACK], BF16, name="ybf%d" % c, align_bytes=64) for c in range(4)]
         o_c = keep.tile([P, U], U32, name="o_c", align_bytes=64)
-        o_s = keep.tile([P, U], U8, name="o_s", align_bytes=64)
+        o_s = keep.tile([P, U // 2], U8, name="o_s", align_bytes=64)
 
         def square(t):
             for acc, entries in banks[t]:
@@ -256,7 +256,8 @@ def tile_picked_sadam_none_po_kernel(
 
         def quantise(c):
             cols = slice(c * CHUNK, (c + 1) * CHUNK)
-            nc.vector.quantize_mx(out=o_c[:, cols].bitcast(FP8X4), scales=o_s[:, cols], in_=y_bf[c][:])
+            scales = o_s[c // 2 * SCALE_ROWS :, chunk(c)]
+            nc.vector.quantize_mx(out=o_c[:, cols].bitcast(FP8X4), scales=scales, in_=y_bf[c][:])
             nc.sync.dma_start(out=words[:, cols], in_=o_c[:, cols].bitcast(I32))
 
         for c in range(2):
@@ -269,4 +270,5 @@ def tile_picked_sadam_none_po_kernel(
             quantise(c)
         for q in range(QUADRANTS):
             queue = nc.scalar if q % 2 == 0 else nc.sync
-            queue.dma_start(out=out_2[0, scale_rows(q), :].bitcast(I32), in_=o_s[scale_partitions(q), :].bitcast(I32))
+            rows = out_2[0, scale_rows(q), :].bitcast(I32).rearrange("r (s c) -> s r c", s=2)
+            queue.dma_start(out=rows, in_=o_s[QUADRANT * q : QUADRANT * q + 2 * SCALE_ROWS, :].bitcast(I32))

@@ -17,6 +17,7 @@ ACT = mybir.ActivationFunctionType
 
 P = 128
 PACK = 4
+PLANE = (0, 2, 3, 1)
 LAST = PACK - 1
 QUADRANT = 32
 QUADRANTS = P // QUADRANT
@@ -26,6 +27,8 @@ LIST_COLS = S // 16
 W_SPLIT = 104
 CHUNK = 256
 PLACE = 4 * S
+HALVES = [slice(h * S // 2, (h + 1) * S // 2) for h in range(2)]
+HALF_LISTS = [slice(h * LIST_COLS // 2, (h + 1) * LIST_COLS // 2) for h in range(2)]
 
 
 def scale_partitions(q):
@@ -74,16 +77,13 @@ def tile_picked_sadam_none_po_kernel(
         def placed(name, shape, dtype, place):
             return work.tile(shape, dtype, name=name, offset=int(place * PLACE), align_bytes=64)
 
-        new_t = [placed("new%d" % t, [P, U], F32, 20 + 2 * t) for t in range(PACK)]
-        m1_t = [placed("m1_%d" % t, [P, U], F32, at) for t, at in enumerate((49, 30, 32, 34))]
-        m2_t = [placed("m2_%d" % t, [P, U], F32, at) for t, at in enumerate((36, 42, 38, 40))]
+        new_t = [placed("new%d" % t, [P, U], F32, 12 + 2 * t) for t in range(PACK)]
+        m1_t = [placed("m1_%d" % t, [P, U], F32, at) for t, at in enumerate((22, 27, 32, 35))]
+        m2_t = [placed("m2_%d" % t, [P, U], F32, at) for t, at in enumerate((20, 24, 30, 38))]
         par_rows = par.rearrange("(p t) u -> p t u", t=PACK)
         m1_rows = m1.rearrange("(p t) u -> p t u", t=PACK)
         m2_rows = m2.rearrange("(p t) u -> p t u", t=PACK)
         out_rows = out_0.rearrange("(p t) u -> p t u", t=PACK)
-
-        def load(tiles, rows, t):
-            nc.sync.dma_start(out=tiles[t][:], in_=rows[:, t, :])
 
         for tiles, rows, t in (
             (m2_t, m2_rows, 0),
@@ -99,7 +99,7 @@ def tile_picked_sadam_none_po_kernel(
             (new_t, par_rows, 3),
             (m2_t, m2_rows, 3),
         ):
-            load(tiles, rows, t)
+            nc.sync.dma_start(out=tiles[t][:], in_=rows[:, PLANE[t], :])
 
         w_bf = keep.tile([P, PACK * P * PACK], BF16, name="w_bf", align_bytes=64)
         w_dst = w_bf[:].rearrange("p (t m j) -> p m j t", t=PACK, j=PACK)
@@ -112,74 +112,65 @@ def tile_picked_sadam_none_po_kernel(
 
         xq_c = keep.tile([P, S], U32, name="xq_c", align_bytes=64)
         for h in range(2):
-            half = slice(h * S // 2, (h + 1) * S // 2)
-            half_list = slice(h * LIST_COLS // 2, (h + 1) * LIST_COLS // 2)
-            nc.vector.tensor_copy(xq_c[:, half], xw[:].bitcast(U32).indirect(offs_t[:, half_list]))
+            nc.vector.tensor_copy(xq_c[:, HALVES[h]], xw[:].bitcast(U32).indirect(offs_t[:, HALF_LISTS[h]]))
 
-        banks = []
-        for t in range(PACK):
-            features = slice(t * P, (t + 1) * P)
-            parts = 2 if t == 0 else 1
-            width = S // parts
-            plane_banks = []
-            for h in range(parts):
-                acc = psum.tile([P, width], F32, name="acc%d_%d" % (t, h))
-                entries = slice(h * width, (h + 1) * width)
-                nc.tensor.matmul_mx(
-                    out=acc[:],
-                    lhsT=w_c[:, features].bitcast(FP8X4),
-                    lhsT_scale=w_s[:, features],
-                    rhs=xq_c[:, entries].bitcast(FP8X4),
-                    rhs_scale=xq_s[:, entries],
-                    start=True,
-                    stop=True,
-                )
-                plane_banks.append((acc, entries))
-            banks.append(plane_banks)
+        def product(name, codes, scales, entries):
+            acc = psum.tile([P, entries.stop - entries.start], F32, name=name)
+            nc.tensor.matmul_mx(
+                out=acc[:],
+                lhsT=codes.bitcast(FP8X4),
+                lhsT_scale=scales,
+                rhs=xq_c[:, entries].bitcast(FP8X4),
+                rhs_scale=xq_s[:, entries],
+                start=True,
+                stop=True,
+            )
+            return acc
+
+        y0 = [product("y0_%d" % h, w_c[:, :P], w_s[:, :P], HALVES[h]) for h in range(2)]
+        y = {}
+        for t in range(1, PACK):
+            features = slice(PLANE[t] * P, (PLANE[t] + 1) * P)
+            y[t] = product("y%d" % t, w_c[:, features], w_s[:, features], slice(0, S))
 
         def picked(name, places):
             return {t: placed(name + str(t), [P, S], F32, at) for t, at in places}
 
-        m1_g = picked("m1g", ((0, 1), (1, 7), (2, 2), (3, 5)))
-        m2_g = picked("m2g", ((0, 9), (1, 51), (2, 17), (3, 12.5)))
-        y_sq7 = picked("ysq", ((0, 6), (1, 8), (2, 28), (3, 29)))
-        r_t = picked("r", ((0, 0), (1, 30), (2, 35), (3, 44)))
-        b_t = picked("b", ((0, 3), (1, 4), (2, 15), (3, 6)))
-        par_g = picked("parg", ((1, 10), (2, 16), (3, 40)))
-        a_t = picked("a", ((0, 45), (1, 18), (2, 19), (3, 10)))
-        u_t = picked("u", ((0, 52), (1, 46), (2, 47), (3, 48)))
-        g_t = [keep.tile([P, S], F32, name="g%d" % t) for t in range(LAST)]
-        pairs = [placed("pairs%d" % s, [P, 2, U // 2, 2], BF16, 11 + 2 * s) for s in range(2)]
+        m1_g = picked("m1g", ((0, 1), (1, 2), (2, 41), (3, 48)))
+        m2_g = picked("m2g", ((0, 3), (1, 42), (2, 43)))
+        y_sq7 = picked("ysq", ((0, 4), (1, 5), (2, 6), (3, 7)))
+        b_t = picked("b", ((0, 8), (1, 9), (2, 10)))
+        r_t = picked("r", ((0, 0), (1, 27), (2, 35)))
+        a_t = picked("a", ((0, 11), (1, 44), (2, 46), (3, 51)))
+        u_t = picked("u", ((0, 52), (1, 52), (2, 47), (3, 55)))
+        par_g = picked("parg", ((1, 53), (2, 49), (3, 39)))
+        g_t = picked("g", ((0, 54), (1, 45), (2, 50)))
+        rounded = keep.tile([P, PACK * U], BF16, name="rounded", align_bytes=64)
+        sides = [rounded[:, 2 * U * s : 2 * U * (s + 1)] for s in range(2)]
+        pairs = [side.rearrange("p (h c e) -> p h c e", h=2, e=2) for side in sides]
+        m2_g[LAST] = rounded[:, :U].bitcast(F32)
+        b_t[LAST] = rounded[:, 3 * U // 2 : 5 * U // 2].bitcast(F32)
+        r_t[LAST] = rounded[:, 3 * U :].bitcast(F32)
         y_bf = [keep.tile([P, CHUNK * PACK], BF16, name="ybf%d" % c, align_bytes=64) for c in range(4)]
         o_c = keep.tile([P, U], U32, name="o_c", align_bytes=64)
         o_s = keep.tile([P, U // 2], U8, name="o_s", align_bytes=64)
 
         def square(t):
-            for acc, entries in banks[t]:
-                nc.scalar.activation(y_sq7[t][:, entries], acc[:], ACT.Square, scale=root[:])
+            nc.scalar.activation(y_sq7[t][:], y[t][:], ACT.Square, scale=root[:])
 
         def first_moment(t):
             sign, op = (-1.0, ALU.subtract) if t == LAST else (1.0, ALU.add)
-            for acc, entries in banks[t]:
-                nc.vector.scalar_tensor_tensor(
-                    a_t[t][:, entries], acc[:], sign * 0.25 / 0.75, m1_g[t][:, entries], ALU.mult, op
-                )
+            nc.vector.scalar_tensor_tensor(a_t[t][:], y[t][:], sign * 0.25 / 0.75, m1_g[t][:], ALU.mult, op)
 
         def inverse_root(t):
             nc.scalar.activation(r_t[t][:], b_t[t][:], ACT.Abs_reciprocal_sqrt, scale=0.875 / (0.5 * 0.75) ** 2)
 
-        def fetch_on_vector(picked, table):
-            nc.vector.tensor_copy(picked[:], table[:].indirect(ent_t[:]))
-
-        def fetch_on_scalar(picked, table):
-            nc.scalar.activation(picked[:], table[:].indirect(ent_t[:]), ACT.Copy)
+        def fetch(dst, table):
+            nc.scalar.activation(dst[:], table[:].indirect(ent_t[:]), ACT.Copy)
 
         def put_back(t):
             nc.vector.tensor_copy(new_t[t][:].indirect(ent_t[:]), g_t[t][:])
-            nc.sync.dma_start(out=out_rows[:, t, :], in_=new_t[t][:])
-
-        halves = [slice(h * S // 2, (h + 1) * S // 2) for h in range(2)]
-        half_lists = [slice(h * LIST_COLS // 2, (h + 1) * LIST_COLS // 2) for h in range(2)]
+            nc.sync.dma_start(out=out_rows[:, PLANE[t], :], in_=new_t[t][:])
 
         def second_moment(t):
             nc.gpsimd.tensor_tensor(b_t[t][:], y_sq7[t][:], m2_g[t][:], ALU.add)
@@ -190,66 +181,68 @@ def tile_picked_sadam_none_po_kernel(
         def take_step(t):
             nc.gpsimd.tensor_tensor(g_t[t][:], par_g[t][:], u_t[t][:], ALU.subtract)
 
-        for t in range(PACK):
-            square(t)
-        fetch_on_vector(m2_g[0], m2_t[0])
-        second_moment(0)
-        fetch_on_vector(m2_g[1], m2_t[1])
-        second_moment(1)
+        def columns(t, s):
+            return new_t[t][:, s * U // 2 : (s + 1) * U // 2]
+
+        def round_plane(t):
+            for s in range(2):
+                nc.scalar.copy(out=pairs[s][:, PLANE[t] // 2, :, PLANE[t] % 2], in_=columns(t, s))
+
         for h in range(2):
-            nc.vector.tensor_copy(m1_g[0][:, halves[h]], m1_t[0][:].indirect(ent_t[:, half_lists[h]]))
+            nc.scalar.activation(y_sq7[0][:, HALVES[h]], y0[h][:], ACT.Square, scale=root[:])
+        for t in range(1, PACK):
+            square(t)
+        for t in range(2):
+            nc.vector.tensor_copy(m2_g[t][:], m2_t[t][:].indirect(ent_t[:]))
+            second_moment(t)
+        for h in range(2):
+            nc.vector.tensor_copy(m1_g[0][:, HALVES[h]], m1_t[0][:].indirect(ent_t[:, HALF_LISTS[h]]))
         inverse_root(0)
-        first_moment(0)
-        for half in halves:
+        for h in range(2):
+            half = HALVES[h]
+            nc.vector.scalar_tensor_tensor(a_t[0][:, half], y0[h][:], 0.25 / 0.75, m1_g[0][:, half], ALU.mult, ALU.add)
+        for half in HALVES:
             nc.vector.tensor_tensor(u_t[0][:, half], a_t[0][:, half], r_t[0][:, half], ALU.mult)
-        fetch_on_scalar(m1_g[1], m1_t[1])
+        fetch(m1_g[1], m1_t[1])
         inverse_root(1)
         first_moment(1)
         nc.vector.tensor_tensor(g_t[0][:], new_t[0][:].indirect(ent_t[:]), u_t[0][:], ALU.subtract)
         put_back(0)
         step(1)
-        fetch_on_scalar(m2_g[2], m2_t[2])
+        fetch(m2_g[2], m2_t[2])
         second_moment(2)
-        fetch_on_scalar(m1_g[2], m1_t[2])
+        fetch(m1_g[2], m1_t[2])
         first_moment(2)
-        fetch_on_scalar(par_g[1], new_t[1])
+        fetch(par_g[1], new_t[1])
         take_step(1)
         put_back(1)
-        fetch_on_scalar(m1_g[3], m1_t[3])
+        fetch(m1_g[3], m1_t[3])
         inverse_root(2)
         step(2)
         first_moment(3)
-        fetch_on_scalar(par_g[2], new_t[2])
+        fetch(par_g[2], new_t[2])
         take_step(2)
         put_back(2)
-        fetch_on_scalar(m2_g[3], m2_t[3])
+        fetch(m2_g[3], m2_t[3])
         second_moment(3)
-        fetch_on_scalar(par_g[3], new_t[3])
+        nc.gpsimd.tensor_scalar(pairs[0][:, 0, :, 0], columns(0, 0), 1.0, 0.0, ALU.mult, ALU.add)
+        fetch(par_g[3], new_t[3])
         inverse_root(3)
         step(3)
         nc.vector.tensor_tensor(new_t[LAST][:].indirect(ent_t[:]), par_g[LAST][:], u_t[LAST][:], ALU.add)
-        nc.sync.dma_start(out=out_rows[:, LAST, :], in_=new_t[LAST][:])
-
-        def columns(t, s):
-            return new_t[t][:, s * U // 2 : (s + 1) * U // 2]
-
-        for t in range(2):
-            for s in range(2):
-                nc.scalar.copy(out=pairs[s][:, 0, :, t], in_=columns(t, s))
-        rounded = pairs[0][:, 1].rearrange("p (h c) e -> p h c e", h=2)
-        source = columns(2, 0).rearrange("p (h c) -> p h c", h=2)
-        nc.scalar.copy(out=rounded[:, :, 2:, 0], in_=source[:, :, 2:])
-        nc.scalar.copy(out=rounded[:, :, :2, :], in_=source[:, :, :2].unsqueeze(3).to_broadcast([P, 2, 2, 2]))
-        nc.scalar.copy(out=pairs[1][:, 1, :, 0], in_=columns(2, 1))
+        nc.sync.dma_start(out=out_rows[:, PLANE[LAST], :], in_=new_t[LAST][:])
+        nc.scalar.copy(out=pairs[1][:, 0, :, 0], in_=columns(0, 1))
+        round_plane(1)
+        round_plane(2)
 
         def chunk(c):
             return slice(c % 2 * CHUNK, (c % 2 + 1) * CHUNK)
 
         def round_last(c, copy):
-            copy(out=pairs[c // 2][:, 1, chunk(c), 1], in_=columns(LAST, c // 2)[:, chunk(c)])
+            copy(out=pairs[c // 2][:, PLANE[LAST] // 2, chunk(c), PLANE[LAST] % 2], in_=columns(LAST, c // 2)[:, chunk(c)])
 
         def weave(c, copy, word):
-            both = pairs[c // 2][:].bitcast(word).rearrange("p h c e -> p c (h e)")
+            both = sides[c // 2].bitcast(word).rearrange("p (h c) -> p c h", h=2)
             copy(out=y_bf[c][:].bitcast(word).rearrange("p (c h) -> p c h", h=2), in_=both[:, chunk(c), :])
 
         words = out_1[0].rearrange("p c r -> p (c r)").bitcast(I32)

@@ -142,13 +142,14 @@ def tile_picked_sadam_none_po_kernel(
         b_t = picked("b", ((0, 8), (1, 9), (2, 10)))
         r_t = picked("r", ((0, 0), (1, 27), (2, 35)))
         a_t = picked("a", ((0, 11), (1, 44), (2, 46), (3, 51)))
-        u_t = picked("u", ((0, 52), (1, 52), (2, 47), (3, 55)))
+        u_t = picked("u", ((0, 52), (2, 47), (3, 55)))
         par_g = picked("parg", ((1, 53), (2, 49), (3, 39)))
         g_t = picked("g", ((0, 54), (1, 45), (2, 50)))
         rounded = keep.tile([P, PACK * U], BF16, name="rounded", align_bytes=64)
         sides = [rounded[:, 2 * U * s : 2 * U * (s + 1)] for s in range(2)]
         pairs = [side.rearrange("p (h c e) -> p h c e", h=2, e=2) for side in sides]
-        m2_g[LAST] = rounded[:, :U].bitcast(F32)
+        u_t[1] = rounded[:, :U].bitcast(F32)
+        m2_g[LAST] = rounded[:, U // 2 : 3 * U // 2].bitcast(F32)
         b_t[LAST] = rounded[:, 3 * U // 2 : 5 * U // 2].bitcast(F32)
         r_t[LAST] = rounded[:, 3 * U :].bitcast(F32)
         y_bf = [keep.tile([P, CHUNK * PACK], BF16, name="ybf%d" % c, align_bytes=64) for c in range(4)]
@@ -184,6 +185,10 @@ def tile_picked_sadam_none_po_kernel(
         def columns(t, s):
             return new_t[t][:, s * U // 2 : (s + 1) * U // 2]
 
+        def round_first(c):
+            cols = slice(c * CHUNK, (c + 1) * CHUNK)
+            nc.gpsimd.tensor_scalar(pairs[0][:, 0, cols, 0], columns(0, 0)[:, cols], 1.0, 0.0, ALU.mult, ALU.add)
+
         def round_plane(t):
             for s in range(2):
                 nc.scalar.copy(out=pairs[s][:, PLANE[t] // 2, :, PLANE[t] % 2], in_=columns(t, s))
@@ -215,6 +220,7 @@ def tile_picked_sadam_none_po_kernel(
         first_moment(2)
         fetch(par_g[1], new_t[1])
         take_step(1)
+        round_first(0)
         put_back(1)
         fetch(m1_g[3], m1_t[3])
         inverse_root(2)
@@ -225,7 +231,7 @@ def tile_picked_sadam_none_po_kernel(
         put_back(2)
         fetch(m2_g[3], m2_t[3])
         second_moment(3)
-        nc.gpsimd.tensor_scalar(pairs[0][:, 0, :, 0], columns(0, 0), 1.0, 0.0, ALU.mult, ALU.add)
+        round_first(1)
         fetch(par_g[3], new_t[3])
         inverse_root(3)
         step(3)

from contextlib import ExitStack

import concourse.mybir as mybir

K, T, S, N, U = 512, 2048, 512, 512, 1024
FLOPS = 2 * K * N * S

F32 = mybir.dt.float32
BF16 = mybir.dt.bfloat16
I32 = mybir.dt.int32
U32 = mybir.dt.uint32
U16 = mybir.dt.uint16
U8 = mybir.dt.uint8
FP8X4 = mybir.dt.float8_e4m3fn_x4
ALU = mybir.AluOpType
ACT = mybir.ActivationFunctionType

P = 128
PACK = 4
PLANE = (0, 2, 3, 1)
LAST = PACK - 1
QUADRANT = 32
QUADRANTS = P // QUADRANT
SCALE_ROWS = 4
TOP = P - QUADRANTS * SCALE_ROWS
LIST_COLS = S // 16
W_SPLIT = 104
CHUNK = 256
PLACE = 4 * S
HALVES = [slice(h * S // 2, (h + 1) * S // 2) for h in range(2)]
HALF_LISTS = [slice(h * LIST_COLS // 2, (h + 1) * LIST_COLS // 2) for h in range(2)]


def scale_partitions(q):
    return slice(QUADRANT * q, QUADRANT * q + SCALE_ROWS)


def scale_rows(q):
    return slice(SCALE_ROWS * q, SCALE_ROWS * (q + 1))


def tile_picked_sadam_none_po_kernel(
    tc, x_words, x_scales, w1, par, m1, m2, offs, ent, out_0, out_1, out_2
):
    nc = tc.nc
    with ExitStack() as ctx:
        keep = ctx.enter_context(tc.tile_pool(name="keep", bufs=1))
        psum = ctx.enter_context(tc.psum_pool(name="psum", bufs=1))

        offs_t = keep.tile([P, LIST_COLS], U16, name="offs_t")
        ent_t = keep.tile([P, LIST_COLS], U16, name="ent_t")
        xw = keep.tile([P, T], I32, name="xw")
        w_raw = keep.tile([P, PACK, N], F32, name="w_raw")
        xg_s = keep.tile([P, S], U8, name="xg_s", align_bytes=64)
        xq_s = keep.tile([P, S], U8, name="xq_s", align_bytes=64)
        seven = keep.tile([P, 1], F32, name="seven")
        root = keep.tile([P, 1], F32, name="root")

        with tc.tile_pool(name="head", bufs=1) as head:
            xs = head.tile([P, T], U8, name="xs")
            nc.sync.dma_start(offs_t[:], offs)
            nc.scalar.dma_start(out=xs[TOP:, :].bitcast(I32), in_=x_scales[0].bitcast(I32))
            nc.sync.dma_start(out=w_raw[:], in_=w1.rearrange("(p j) c -> p j c", j=PACK))
            nc.sync.dma_start(out=xw[:], in_=x_words[0].rearrange("p c r -> p (c r)").bitcast(I32))
            nc.sync.dma_start(ent_t[:], ent)
            nc.vector.memset(xs[:TOP, :].bitcast(I32), 0)
            nc.vector.memset(seven[:], 7.0)
            nc.vector.memset(xq_s[:].bitcast(I32), 0)
            nc.scalar.activation(root[:], seven[:], ACT.Abs_reciprocal_sqrt)
            nc.vector.tensor_copy(xg_s[:], xs[:].indirect(offs_t[:]))
        for q in range(QUADRANTS):
            picked = slice(TOP + SCALE_ROWS * q, TOP + SCALE_ROWS * (q + 1))
            nc.sync.dma_start(out=xq_s[scale_partitions(q), :].bitcast(I32), in_=xg_s[picked, :].bitcast(I32))

        work = ctx.enter_context(tc.tile_pool(name="work", bufs=1))

        def placed(name, shape, dtype, place):
            return work.tile(shape, dtype, name=name, offset=int(place * PLACE), align_bytes=64)

        new_t = [placed("new%d" % t, [P, U], F32, 12 + 2 * t) for t in range(PACK)]
        m1_t = [placed("m1_%d" % t, [P, U], F32, at) for t, at in enumerate((22, 27, 32, 35))]
        m2_t = [placed("m2_%d" % t, [P, U], F32, at) for t, at in enumerate((20, 24, 30, 38))]
        par_rows = par.rearrange("(p t) u -> p t u", t=PACK)
        m1_rows = m1.rearrange("(p t) u -> p t u", t=PACK)
        m2_rows = m2.rearrange("(p t) u -> p t u", t=PACK)
        out_rows = out_0.rearrange("(p t) u -> p t u", t=PACK)

        for tiles, rows, t in (
            (m2_t, m2_rows, 0),
            (m2_t, m2_rows, 1),
            (m1_t, m1_rows, 0),
            (m1_t, m1_rows, 1),
            (new_t, par_rows, 0),
            (m2_t, m2_rows, 2),
            (m1_t, m1_rows, 2),
            (new_t, par_rows, 1),
            (m1_t, m1_rows, 3),
            (new_t, par_rows, 2),
            (new_t, par_rows, 3),
            (m2_t, m2_rows, 3),
        ):
            nc.sync.dma_start(out=tiles[t][:], in_=rows[:, PLANE[t], :])

        w_bf = keep.tile([P, PACK * P * PACK], BF16, name="w_bf", align_bytes=64)
        w_dst = w_bf[:].rearrange("p (t m j) -> p m j t", t=PACK, j=PACK)
        w_src = w_raw[:].rearrange("p j (m t) -> p m j t", t=PACK)
        nc.vector.tensor_copy(out=w_dst[:, :W_SPLIT], in_=w_src[:, :W_SPLIT])
        nc.scalar.copy(out=w_dst[:, W_SPLIT:], in_=w_src[:, W_SPLIT:])
        w_c = placed("w_c", [P, N], U32, 0)
        w_s = keep.tile([P, N], U8, name="w_s", align_bytes=64)
        nc.vector.quantize_mx(out=w_c[:].bitcast(FP8X4), scales=w_s[:], in_=w_bf[:])

        xq_c = keep.tile([P, S], U32, name="xq_c", align_bytes=64)
        for h in range(2):
            nc.vector.tensor_copy(xq_c[:, HALVES[h]], xw[:].bitcast(U32).indirect(offs_t[:, HALF_LISTS[h]]))

        def product(name, codes, scales, entries):
            acc = psum.tile([P, entries.stop - entries.start], F32, name=name)
            nc.tensor.matmul_mx(
                out=acc[:],
                lhsT=codes.bitcast(FP8X4),
                lhsT_scale=scales,
                rhs=xq_c[:, entries].bitcast(FP8X4),
                rhs_scale=xq_s[:, entries],
                start=True,
                stop=True,
            )
            return acc

        y0 = [product("y0_%d" % h, w_c[:, :P], w_s[:, :P], HALVES[h]) for h in range(2)]
        y = {}
        for t in range(1, PACK):
            features = slice(PLANE[t] * P, (PLANE[t] + 1) * P)
            y[t] = product("y%d" % t, w_c[:, features], w_s[:, features], slice(0, S))

        def picked(name, places):
            return {t: placed(name + str(t), [P, S], F32, at) for t, at in places}

        m1_g = picked("m1g", ((0, 1), (1, 2), (2, 41), (3, 48)))
        m2_g = picked("m2g", ((0, 3), (1, 42), (2, 43)))
        y_sq7 = picked("ysq", ((0, 4), (1, 5), (2, 6), (3, 7)))
        b_t = picked("b", ((0, 8), (1, 9), (2, 10)))
        r_t = picked("r", ((0, 0), (1, 27), (2, 35)))
        a_t = picked("a", ((0, 11), (1, 44), (2, 46), (3, 51)))
        u_t = picked("u", ((0, 52), (2, 47), (3, 55)))
        par_g = picked("parg", ((1, 53), (2, 49), (3, 39)))
        g_t = picked("g", ((0, 54), (1, 45), (2, 50)))
        rounded = keep.tile([P, PACK * U], BF16, name="rounded", align_bytes=64)
        sides = [rounded[:, 2 * U * s : 2 * U * (s + 1)] for s in range(2)]
        pairs = [side.rearrange("p (h c e) -> p h c e", h=2, e=2) for side in sides]
        u_t[1] = rounded[:, :U].bitcast(F32)
        m2_g[LAST] = rounded[:, U // 2 : 3 * U // 2].bitcast(F32)
        b_t[LAST] = rounded[:, 3 * U // 2 : 5 * U // 2].bitcast(F32)
        r_t[LAST] = rounded[:, 3 * U :].bitcast(F32)
        y_bf = [keep.tile([P, CHUNK * PACK], BF16, name="ybf%d" % c, align_bytes=64) for c in range(4)]
        o_c = keep.tile([P, U], U32, name="o_c", align_bytes=64)
        o_s = keep.tile([P, U // 2], U8, name="o_s", align_bytes=64)

        def square(t):
            nc.scalar.activation(y_sq7[t][:], y[t][:], ACT.Square, scale=root[:])

        def first_moment(t):
            sign, op = (-1.0, ALU.subtract) if t == LAST else (1.0, ALU.add)
            nc.vector.scalar_tensor_tensor(a_t[t][:], y[t][:], sign * 0.25 / 0.75, m1_g[t][:], ALU.mult, op)

        def inverse_root(t):
            nc.scalar.activation(r_t[t][:], b_t[t][:], ACT.Abs_reciprocal_sqrt, scale=0.875 / (0.5 * 0.75) ** 2)

        def fetch(dst, table):
            nc.scalar.activation(dst[:], table[:].indirect(ent_t[:]), ACT.Copy)

        def put_back(t):
            nc.vector.tensor_copy(new_t[t][:].indirect(ent_t[:]), g_t[t][:])
            nc.sync.dma_start(out=out_rows[:, PLANE[t], :], in_=new_t[t][:])

        def second_moment(t):
            nc.gpsimd.tensor_tensor(b_t[t][:], y_sq7[t][:], m2_g[t][:], ALU.add)

        def step(t):
            nc.gpsimd.tensor_tensor(u_t[t][:], a_t[t][:], r_t[t][:], ALU.mult)

        def take_step(t):
            nc.gpsimd.tensor_tensor(g_t[t][:], par_g[t][:], u_t[t][:], ALU.subtract)

        def columns(t, s):
            return new_t[t][:, s * U // 2 : (s + 1) * U // 2]

        def round_first(c):
            cols = slice(c * CHUNK, (c + 1) * CHUNK)
            nc.gpsimd.tensor_scalar(pairs[0][:, 0, cols, 0], columns(0, 0)[:, cols], 1.0, 0.0, ALU.mult, ALU.add)

        def round_plane(t):
            for s in range(2):
                nc.scalar.copy(out=pairs[s][:, PLANE[t] // 2, :, PLANE[t] % 2], in_=columns(t, s))

        for h in range(2):
            nc.scalar.activation(y_sq7[0][:, HALVES[h]], y0[h][:], ACT.Square, scale=root[:])
        for t in range(1, PACK):
            square(t)
        for t in range(2):
            nc.vector.tensor_copy(m2_g[t][:], m2_t[t][:].indirect(ent_t[:]))
            second_moment(t)
        for h in range(2):
            nc.vector.tensor_copy(m1_g[0][:, HALVES[h]], m1_t[0][:].indirect(ent_t[:, HALF_LISTS[h]]))
        inverse_root(0)
        for h in range(2):
            half = HALVES[h]
            nc.vector.scalar_tensor_tensor(a_t[0][:, half], y0[h][:], 0.25 / 0.75, m1_g[0][:, half], ALU.mult, ALU.add)
        for half in HALVES:
            nc.vector.tensor_tensor(u_t[0][:, half], a_t[0][:, half], r_t[0][:, half], ALU.mult)
        fetch(m1_g[1], m1_t[1])
        inverse_root(1)
        first_moment(1)
        nc.vector.tensor_tensor(g_t[0][:], new_t[0][:].indirect(ent_t[:]), u_t[0][:], ALU.subtract)
        put_back(0)
        step(1)
        fetch(m2_g[2], m2_t[2])
        second_moment(2)
        fetch(m1_g[2], m1_t[2])
        first_moment(2)
        fetch(par_g[1], new_t[1])
        take_step(1)
        round_first(0)
        put_back(1)
        fetch(m1_g[3], m1_t[3])
        inverse_root(2)
        step(2)
        first_moment(3)
        fetch(par_g[2], new_t[2])
        take_step(2)
        put_back(2)
        fetch(m2_g[3], m2_t[3])
        second_moment(3)
        round_first(1)
        fetch(par_g[3], new_t[3])
        inverse_root(3)
        step(3)
        nc.vector.tensor_tensor(new_t[LAST][:].indirect(ent_t[:]), par_g[LAST][:], u_t[LAST][:], ALU.add)
        nc.sync.dma_start(out=out_rows[:, PLANE[LAST], :], in_=new_t[LAST][:])
        nc.scalar.copy(out=pairs[1][:, 0, :, 0], in_=columns(0, 1))
        round_plane(1)
        round_plane(2)

        def chunk(c):
            return slice(c % 2 * CHUNK, (c % 2 + 1) * CHUNK)

        def round_last(c, copy):
            copy(out=pairs[c // 2][:, PLANE[LAST] // 2, chunk(c), PLANE[LAST] % 2], in_=columns(LAST, c // 2)[:, chunk(c)])

        def weave(c, copy, word):
            both = sides[c // 2].bitcast(word).rearrange("p (h c) -> p c h", h=2)
            copy(out=y_bf[c][:].bitcast(word).rearrange("p (c h) -> p c h", h=2), in_=both[:, chunk(c), :])

        words = out_1[0].rearrange("p c r -> p (c r)").bitcast(I32)

        def quantise(c):
            cols = slice(c * CHUNK, (c + 1) * CHUNK)
            scales = o_s[c // 2 * SCALE_ROWS :, chunk(c)]
            nc.vector.quantize_mx(out=o_c[:, cols].bitcast(FP8X4), scales=scales, in_=y_bf[c][:])
            nc.sync.dma_start(out=words[:, cols], in_=o_c[:, cols].bitcast(I32))

        for c in range(2):
            round_last(c, nc.vector.tensor_copy)
            round_last(c + 2, nc.scalar.copy)
        for c in range(2):
            weave(c, nc.vector.tensor_copy, I32)
            weave(c + 2, nc.scalar.copy, U32)
        for c in range(4):
            quantise(c)
        for q in range(QUADRANTS):
            queue = nc.scalar if q % 2 == 0 else nc.sync
            rows = out_2[0, scale_rows(q), :].bitcast(I32).rearrange("r (s c) -> s r c", s=2)
            queue.dma_start(out=rows, in_=o_s[QUADRANT * q : QUADRANT * q + 2 * SCALE_ROWS, :].bitcast(I32))
